import numpy as np
import ml_dtypes


def mxq(x, axis, fmt="e4m3"):
    dtype, down = {"e4m3": (ml_dtypes.float8_e4m3fn, 7), "e5m2": (ml_dtypes.float8_e5m2, 14)}[fmt]
    v = np.moveaxis(np.asarray(x, np.float32).astype(ml_dtypes.bfloat16).astype(np.float64), axis, -1)
    blocks = v.reshape(v.shape[:-1] + (-1, 32))
    amax = np.abs(blocks).max(-1, keepdims=True)
    byte = np.maximum(np.where(amax > 0, np.frexp(amax)[1] - 1 + 127, 0) - down, 1)
    scale = np.exp2(byte - 127.0)
    codes = (blocks / scale).astype(np.float32).astype(dtype).astype(np.float64)
    return np.moveaxis((codes * scale).reshape(v.shape), -1, axis)


WIDE = False


def mx_kscale(k):
    if not WIDE:
        return np.ones(k)
    levels = np.array([24, -24, 12, -12, 0])
    if k % 512:
        return np.exp2(np.random.permutation(np.resize(levels, k // 32))).repeat(32)
    a = np.empty((k // 512, 16))
    for p in range(k // 512):
        a[p, :8] = np.random.permutation(np.resize(levels, 8))
        for g in range(8):
            far = levels[np.abs(levels - a[p, g]) >= 10]
            a[p, g + 8] = far[np.random.randint(len(far))]
    return np.exp2(a.ravel()).repeat(32)


def f64(x):
    return np.asarray(x).astype(np.float64)


def striped(idx):
    return np.tile(idx.reshape(-1, 16).T, (8, 1)).astype(np.uint16)


def unstriped(offs):
    return offs[:16].T.reshape(-1).astype(np.int64)


E2M1 = np.array([0.0, 0.5, 1.0, 1.5, 2.0, 3.0, 4.0, 6.0, -0.0, -0.5, -1.0, -1.5, -2.0, -3.0, -4.0, -6.0])


def pack_weight(w, fmt):
    k, n = w.shape
    w = f64(np.asarray(w, np.float32).astype(ml_dtypes.bfloat16)).reshape(k // 32, 32, n)
    amax = np.abs(w).max(1)
    if fmt == "e4m3":
        byte = np.frexp(amax)[1] - 1 + 127 - 7
    else:
        mant, ex = np.frexp(amax / 6.0)
        byte = np.where(mant > 0.5, ex, ex - 1) + 127
    byte = np.clip(np.where(amax > 0, byte, 1), 1, 254)
    scaled = (w * np.exp2(127.0 - byte)[:, None, :]).reshape(k, n).astype(np.float32)
    by_word = np.ascontiguousarray(scaled.reshape(k // 512, 128, 4, n).transpose(0, 1, 3, 2))
    if fmt == "e4m3":
        words = by_word.astype(ml_dtypes.float8_e4m3fn).view(np.uint8)
    else:
        c = by_word.astype(ml_dtypes.float4_e2m1fn).view(np.uint8) & 0xF
        words = (c[..., 0::2] | (c[..., 1::2] << 4)).reshape(k // 512, 128, 2 * n)
    return np.ascontiguousarray(words), np.ascontiguousarray(byte.astype(np.uint8).reshape(k // 512, 16, n))


def unpack_weight(words, scales, fmt):
    g, _, n = scales.shape
    words = np.ascontiguousarray(words).reshape(g, 128, n, -1)
    if fmt == "e4m3":
        vals = words.view(ml_dtypes.float8_e4m3fn).astype(np.float64)
    else:
        nib = np.empty((g, 128, n, 4), np.uint8)
        nib[..., 0::2] = words & 0xF
        nib[..., 1::2] = words >> 4
        vals = E2M1[nib]
    vals = vals * np.repeat(np.exp2(scales.astype(np.float64) - 127.0), 8, axis=1)[..., None]
    return vals.transpose(0, 1, 3, 2).reshape(g * 512, n)


def pack_table4(v):
    words, scales = pack_weight(v, "e2m1")
    g, t = words.shape[0] // 2, v.shape[1]
    return np.ascontiguousarray(words.reshape(g, 2, 128, t, 2).transpose(0, 2, 3, 1, 4).reshape(g, 128, t, 4)), scales


def unpack_table4(words, scales):
    g, _, t, _ = words.shape
    return unpack_weight(words.reshape(g, 128, t, 2, 2).transpose(0, 3, 1, 2, 4).reshape(2 * g, 128, 2 * t), scales, "e2m1")


def planes(y):
    n, m = y.shape
    v = y.astype(np.float32).astype(ml_dtypes.bfloat16).astype(np.float64).reshape(n // 32, 32, m)
    top = np.abs(v).max(1)
    byte = np.clip(np.where(top > 0, np.frexp(top)[1] - 1 + 127 - 7, 1), 1, 254)
    codes = (v * np.exp2(127.0 - byte)[:, None, :]).reshape(n, m).astype(np.float32).astype(ml_dtypes.float8_e4m3fn).view(np.uint8)
    words = codes.reshape(n // 512, 128, 4, m).transpose(0, 1, 3, 2)
    return np.ascontiguousarray(words), np.ascontiguousarray(byte.astype(np.uint8).reshape(n // 512, 16, m))


K, N, T, J = 1024, 512, 4096, 1024


def setup_inputs():
    n = np.random.standard_normal
    s = mx_kscale(K)[:, None]
    p_tab = pack_table4(n((K, T)) * s)
    p_wk = pack_weight(n((K, N)) / np.sqrt(K) / s, "e4m3")
    p_wv4 = pack_weight(n((K, N)) / np.sqrt(K) / s, "e2m1")
    return {
        "tab_words": p_tab[0],
        "tab_scales": p_tab[1],
        "wk_words": p_wk[0],
        "wk_scales": p_wk[1],
        "wv4_words": p_wv4[0],
        "wv4_scales": p_wv4[1],
        "wvd": (0.4 * (n((K, N)) / np.sqrt(K) / s)).astype(np.float32),
        "st": (n((N, J))).astype(np.float32),
        "rT": (n((N, T))).astype(np.float32),
        "offs": striped(np.random.permutation(T)[:J]),
    }


def reference(tab_words, tab_scales, wk_words, wk_scales, wv4_words, wv4_scales, wvd, st, rT, offs):
    idx = unstriped(offs)
    tab_ = unpack_table4(tab_words, tab_scales)[:, idx]
    wk_ = unpack_weight(wk_words, wk_scales, "e4m3")
    wv4_ = unpack_weight(wv4_words, wv4_scales, "e2m1")
    wvd_ = mxq(f64(wvd), 0, "e4m3")
    ke = wk_.T @ tab_
    ve = wv4_.T @ tab_ + wvd_.T @ tab_
    gate = np.tanh(ke * f64(st))
    out_0 = f64(rT)[:, idx] + gate * ve
    return (out_0,) + planes(out_0)

@@ -1,0 +1,191 @@
+from contextlib import ExitStack
+
+import concourse.mybir as mybir
+
+K, N, T, J = 1024, 512, 4096, 1024
+FLOPS = 3 * 2 * K * N * J
+
+F32 = mybir.dt.float32
+BF16 = mybir.dt.bfloat16
+I32 = mybir.dt.int32
+U32 = mybir.dt.uint32
+U16 = mybir.dt.uint16
+U8 = mybir.dt.uint8
+FP8X4 = mybir.dt.float8_e4m3fn_x4
+FP4X4 = mybir.dt.float4_e2m1fn_x4
+MULT = mybir.AluOpType.mult
+ADD = mybir.AluOpType.add
+TANH = mybir.ActivationFunctionType.Tanh
+
+P = 128
+PACK = 4
+PASSES = K // (P * PACK)
+BANK = 512
+ROWS = 16
+CHUNKS = [256, 256, 256, 256]
+WK_COL = J
+WV_COL = J + N
+PLANE = J + 2 * N
+
+
+def tile_list_engram_dl_tanhLP_kernel(
+    tc, tab_words, tab_scales, wk_words, wk_scales, wv4_words, wv4_scales, wvd, st, rT, offs, out_0, out_1, out_2
+):
+    nc = tc.nc
+    with ExitStack() as ctx:
+        keep = ctx.enter_context(tc.tile_pool(name="keep", bufs=1))
+        work = ctx.enter_context(tc.tile_pool(name="work", bufs=4))
+        psum = ctx.enter_context(tc.psum_pool(name="psum", bufs=4))
+
+        offsets = keep.tile([P, J // 16], U16, name="offsets")
+        tab_sc = keep.tile([P, T], U8, name="tab_sc", align_bytes=64)
+        w_sc = keep.tile([P, 2 * N], U8, name="w_sc", align_bytes=64)
+        planes = keep.tile([P, PASSES, PLANE], U8, name="planes", align_bytes=64)
+        tab_raw = keep.tile([P, T], I32, name="tab_raw", align_bytes=64)
+        wk_raw = keep.tile([P, PASSES, N], I32, name="wk_raw", align_bytes=64)
+        wv_raw = keep.tile([P, PASSES, 2 * N], U8, name="wv_raw", align_bytes=64)
+        wd_raw = [keep.tile([P, PACK, N], F32, name="wd_raw%d" % a) for a in range(PASSES)]
+        st_sb = [keep.tile([P, 2, J], F32, name="st_sb%d" % u, tag="pair%d" % u) for u in range(2)]
+        r_sb = [keep.tile([P, T], F32, name="r_sb%d" % t) for t in range(PACK)]
+
+        live = PASSES * ROWS
+        nc.sync.dma_start(offsets[:], offs)
+        nc.sync.dma_start(tab_sc[0:live, :].bitcast(I32), tab_scales.rearrange("a q t -> (a q) t").bitcast(I32))
+        nc.sync.dma_start(w_sc[0:live, 0:N].bitcast(I32), wk_scales.rearrange("a q n -> (a q) n").bitcast(I32))
+        nc.sync.dma_start(w_sc[0:live, N : 2 * N].bitcast(I32), wv4_scales.rearrange("a q n -> (a q) n").bitcast(I32))
+        nc.sync.dma_start(wk_raw[:], wk_words.rearrange("a p n i -> p a (n i)").bitcast(I32))
+        nc.sync.dma_start(wv_raw[:].bitcast(I32), wv4_words.rearrange("a p b -> p a b").bitcast(I32))
+        nc.sync.dma_start(tab_raw[:], tab_words[0].rearrange("p t b -> p (t b)").bitcast(I32))
+        wvd_rows = wvd.rearrange("(a p i) n -> a p i n", a=PASSES, i=PACK)
+        for a in range(PASSES):
+            nc.sync.dma_start(wd_raw[a][:], wvd_rows[a])
+        st_rows = st.rearrange("(p t) j -> p t j", t=PACK)
+        for u in range(2):
+            nc.sync.dma_start(st_sb[u][:], st_rows[:, 2 * u : 2 * u + 2, :])
+        r_rows = rT.rearrange("(p t) c -> p t c", t=PACK)
+        for t in range(PACK):
+            nc.sync.dma_start(r_sb[t][:], r_rows[:, t, :])
+
+        for rows in (slice(32, 64), slice(64, P)):
+            nc.vector.memset(tab_sc[rows, :].bitcast(I32), 0)
+            nc.vector.memset(w_sc[rows, :].bitcast(I32), 0)
+        nc.vector.memset(planes[:].rearrange("p a c -> p (a c)").bitcast(I32), 0)
+
+        picked_sc = keep.tile([P, J], U8, name="picked_sc", align_bytes=64)
+        nc.vector.tensor_copy(picked_sc[:], tab_sc[:].indirect(offsets[:]))
+        all_sc = keep.tile([P, PLANE], U8, name="all_sc", align_bytes=64)
+        nc.vector.tensor_copy(all_sc[:, 0:J].bitcast(I32), picked_sc[:].bitcast(I32))
+        nc.vector.tensor_copy(
+            all_sc[:, J:PLANE].rearrange("p (w t m) -> p w t m", w=2, t=PACK),
+            w_sc[:].rearrange("p (w m t) -> p w t m", w=2, t=PACK),
+        )
+        for a in range(PASSES):
+            for r in range(4):
+                nc.gpsimd.dma_start(
+                    planes[r:P:32, a, :].bitcast(I32),
+                    all_sc[ROWS * a + r : ROWS * (a + 1) : 4, :].bitcast(I32),
+                )
+
+        wk_codes = keep.tile([P, PASSES, N], I32, name="wk_codes", align_bytes=64)
+        nc.vector.tensor_copy(
+            wk_codes[:].rearrange("p a (t g m) -> p a g t m", t=PACK, m=4),
+            wk_raw[:].rearrange("p a (g m t) -> p a g t m", t=PACK, m=4),
+        )
+        wv_codes = keep.tile([P, PASSES, 2 * N], U8, name="wv_codes", align_bytes=64)
+        nc.vector.tensor_copy(
+            wv_codes[:].bitcast(U16).rearrange("p a (t g m) -> p a g t m", t=PACK, m=8),
+            wv_raw[:].bitcast(U16).rearrange("p a (g m t) -> p a g t m", t=PACK, m=8),
+        )
+
+        picked = keep.tile([P, J], U32, name="picked", align_bytes=64)
+        nc.vector.tensor_copy(picked[:], tab_raw[:].bitcast(U32).indirect(offsets[:]))
+        tab_codes = keep.tile([P, PASSES, 2 * J], U8, name="tab_codes", align_bytes=64)
+        nc.vector.tensor_copy(
+            tab_codes[:].bitcast(U16).rearrange("p a (g m) -> p g a m", m=8),
+            picked[:].bitcast(U16).rearrange("p (g m a) -> p g a m", a=PASSES, m=8),
+        )
+
+        wd_codes = [keep.tile([P, N], U32, name="wd_codes%d" % a, align_bytes=64) for a in range(PASSES)]
+        wd_scales = [keep.tile([P, N], U8, name="wd_scales%d" % a, align_bytes=64) for a in range(PASSES)]
+        for a in range(PASSES):
+            wd_bf = keep.tile([P, PACK * N], BF16, name="wd_bf%d" % a, align_bytes=64)
+            nc.scalar.copy(
+                wd_bf[:].rearrange("p (t m i) -> p m t i", t=PACK, i=PACK),
+                wd_raw[a][:].rearrange("p i (m t) -> p m t i", t=PACK),
+            )
+            nc.vector.quantize_mx(out=wd_codes[a][:].bitcast(FP8X4), scales=wd_scales[a][:], in_=wd_bf[:])
+
+        def product(acc, operands, h):
+            count = len(operands) * PASSES
+            step = 0
+            for codes, scales in operands:
+                for a in range(PASSES):
+                    nc.tensor.matmul_mx(
+                        out=acc[:],
+                        lhsT=codes(a),
+                        lhsT_scale=scales(a),
+                        rhs=tab_codes[:, a, 2 * BANK * h : 2 * BANK * (h + 1)].bitcast(FP4X4),
+                        rhs_scale=planes[:, a, BANK * h : BANK * (h + 1)],
+                        start=(step == 0),
+                        stop=(step == count - 1),
+                    )
+                    step = step + 1
+
+        gated = [keep.tile([P, J], F32, name="gated%d" % t) for t in range(PACK)]
+        for t in range(PACK):
+            lo, hi = P * t, P * (t + 1)
+            wk_op = (lambda a: wk_codes[:, a, lo:hi].bitcast(FP8X4), lambda a: planes[:, a, WK_COL + lo : WK_COL + hi])
+            wv_op = (
+                lambda a: wv_codes[:, a, 2 * lo : 2 * hi].bitcast(FP4X4),
+                lambda a: planes[:, a, WV_COL + lo : WV_COL + hi],
+            )
+            wd_op = (lambda a: wd_codes[a][:, lo:hi].bitcast(FP8X4), lambda a: wd_scales[a][:, lo:hi])
+            for h in range(J // BANK):
+                cols = slice(BANK * h, BANK * (h + 1))
+                ke = psum.tile([P, BANK], F32, name="ke")
+                product(ke, [wk_op], h)
+                ve = psum.tile([P, BANK], F32, name="ve")
+                product(ve, [wv_op, wd_op], h)
+                score = work.tile([P, BANK], F32, name="score")
+                nc.vector.tensor_tensor(score[:], ke[:], st_sb[t // 2][:, t % 2, cols], MULT)
+                gate = work.tile([P, BANK], F32, name="gate")
+                nc.scalar.activation(gate[:], score[:], TANH)
+                nc.vector.tensor_tensor(gated[t][:, cols], ve[:], gate[:], MULT)
+
+        y = [keep.tile([P, 2, J], F32, name="y%d" % u, tag="pair%d" % u) for u in range(2)]
+        y_bf = [keep.tile([P, w, PACK], BF16, name="y_bf%d" % c, align_bytes=64) for c, w in enumerate(CHUNKS)]
+        y_codes = keep.tile([P, J], U32, name="y_codes", align_bytes=64)
+        y_scales = keep.tile([P, J], U8, name="y_scales", align_bytes=64)
+        out_rows = out_0.rearrange("(p t) j -> p t j", t=PACK)
+        out_words = out_1[0].rearrange("p j i -> p (j i)").bitcast(I32)
+        starts = [sum(CHUNKS[:c]) for c in range(len(CHUNKS))]
+
+        def round_pair(u, c):
+            cols = slice(starts[c], starts[c] + CHUNKS[c])
+            nc.scalar.copy(y_bf[c][:, :, 2 * u : 2 * u + 2], y[u][:, :, cols].rearrange("p t j -> p j t"))
+
+        for t in range(PACK - 1):
+            nc.vector.tensor_tensor(y[t // 2][:, t % 2, :], r_sb[t][:].indirect(offsets[:]), gated[t][:], ADD)
+            if t == 1:
+                nc.sync.dma_start(out_rows[:, 0:2, :], y[0][:])
+                for c in range(len(CHUNKS)):
+                    round_pair(0, c)
+        nc.sync.dma_start(out_rows[:, 2, :], y[1][:, 0, :])
+        last = PACK - 1
+        for c in range(len(CHUNKS) + 1):
+            if c < len(CHUNKS):
+                cols = slice(starts[c], starts[c] + CHUNKS[c])
+                picks = offsets[:, cols.start // 16 : cols.stop // 16]
+                nc.vector.tensor_tensor(y[1][:, 1, cols], r_sb[last][:].indirect(picks), gated[last][:, cols], ADD)
+                nc.sync.dma_start(out_rows[:, last, cols], y[1][:, 1, cols])
+                round_pair(1, c)
+            if c > 0:
+                cols = slice(starts[c - 1], starts[c - 1] + CHUNKS[c - 1])
+                nc.vector.quantize_mx(
+                    out=y_codes[:, cols].bitcast(FP8X4),
+                    scales=y_scales[:, cols],
+                    in_=y_bf[c - 1][:].rearrange("p j t -> p (j t)"),
+                )
+                nc.sync.dma_start(out_words[:, cols], y_codes[:, cols].bitcast(I32))
+        for q in range(4):
+            nc.scalar.dma_start(out_2[0, 4 * q : 4 * q + 4, :].bitcast(I32), y_scales[32 * q : 32 * q + 4, :].bitcast(I32))

@@ -41,63 +41,45 @@ def tile_list_engram_dl_tanhLP_kernel(
         tab_sc = keep.tile([P, T], U8, name="tab_sc", align_bytes=64)
         w_sc = keep.tile([P, 2 * N], U8, name="w_sc", align_bytes=64)
         planes = keep.tile([P, PASSES, PLANE], U8, name="planes", align_bytes=64)
-        tab_raw = keep.tile([P, T], I32, name="tab_raw", align_bytes=64)
-        wk_raw = keep.tile([P, PASSES, N], I32, name="wk_raw", align_bytes=64)
-        wv_raw = keep.tile([P, PASSES, 2 * N], U8, name="wv_raw", align_bytes=64)
-        wd_raw = [keep.tile([P, PACK, N], F32, name="wd_raw%d" % a) for a in range(PASSES)]
-        st_sb = [keep.tile([P, 2, J], F32, name="st_sb%d" % u, tag="pair%d" % u) for u in range(2)]
-        r_sb = [keep.tile([P, T], F32, name="r_sb%d" % t) for t in range(PACK)]
+        tab_raw = keep.tile([P, T], I32, name="tab_raw", tag="pair0", align_bytes=64)
+        wk_raw = keep.tile([P, PASSES, N], I32, name="wk_raw", tag="pair1", align_bytes=64)
+        wv_raw = keep.tile([P, PASSES, 2 * N], U8, name="wv_raw", tag="wide0", align_bytes=64)
 
         live = PASSES * ROWS
         nc.sync.dma_start(offsets[:], offs)
         nc.sync.dma_start(tab_sc[0:live, :].bitcast(I32), tab_scales.rearrange("a q t -> (a q) t").bitcast(I32))
         nc.sync.dma_start(w_sc[0:live, 0:N].bitcast(I32), wk_scales.rearrange("a q n -> (a q) n").bitcast(I32))
         nc.sync.dma_start(w_sc[0:live, N : 2 * N].bitcast(I32), wv4_scales.rearrange("a q n -> (a q) n").bitcast(I32))
+        nc.sync.dma_start(tab_raw[:], tab_words[0].rearrange("p t b -> p (t b)").bitcast(I32))
         nc.sync.dma_start(wk_raw[:], wk_words.rearrange("a p n i -> p a (n i)").bitcast(I32))
         nc.sync.dma_start(wv_raw[:].bitcast(I32), wv4_words.rearrange("a p b -> p a b").bitcast(I32))
-        nc.sync.dma_start(tab_raw[:], tab_words[0].rearrange("p t b -> p (t b)").bitcast(I32))
-        wvd_rows = wvd.rearrange("(a p i) n -> a p i n", a=PASSES, i=PACK)
-        for a in range(PASSES):
-            nc.sync.dma_start(wd_raw[a][:], wvd_rows[a])
-        st_rows = st.rearrange("(p t) j -> p t j", t=PACK)
-        for u in range(2):
-            nc.sync.dma_start(st_sb[u][:], st_rows[:, 2 * u : 2 * u + 2, :])
-        r_rows = rT.rearrange("(p t) c -> p t c", t=PACK)
-        for t in range(PACK):
-            nc.sync.dma_start(r_sb[t][:], r_rows[:, t, :])
 
         for rows in (slice(32, 64), slice(64, P)):
             nc.vector.memset(tab_sc[rows, :].bitcast(I32), 0)
             nc.vector.memset(w_sc[rows, :].bitcast(I32), 0)
-        nc.vector.memset(planes[:].rearrange("p a c -> p (a c)").bitcast(I32), 0)
+        nc.gpsimd.memset(planes[:].rearrange("p a c -> p (a c)").bitcast(I32), 0)
 
-        picked_sc = keep.tile([P, J], U8, name="picked_sc", align_bytes=64)
-        nc.vector.tensor_copy(picked_sc[:], tab_sc[:].indirect(offsets[:]))
         all_sc = keep.tile([P, PLANE], U8, name="all_sc", align_bytes=64)
-        nc.vector.tensor_copy(all_sc[:, 0:J].bitcast(I32), picked_sc[:].bitcast(I32))
         nc.vector.tensor_copy(
             all_sc[:, J:PLANE].rearrange("p (w t m) -> p w t m", w=2, t=PACK),
             w_sc[:].rearrange("p (w m t) -> p w t m", w=2, t=PACK),
         )
+        picked_sc = keep.tile([P, J], U8, name="picked_sc", tag="wide1", align_bytes=64)
+        nc.vector.tensor_copy(picked_sc[:], tab_sc[:].indirect(offsets[:]))
+        nc.vector.tensor_copy(all_sc[:, 0:J].bitcast(I32), picked_sc[:].bitcast(I32))
         for a in range(PASSES):
             for r in range(4):
-                nc.gpsimd.dma_start(
+                queue = nc.gpsimd if 4 * a + r < 3 else nc.sync
+                queue.dma_start(
                     planes[r:P:32, a, :].bitcast(I32),
                     all_sc[ROWS * a + r : ROWS * (a + 1) : 4, :].bitcast(I32),
                 )
 
-        wk_codes = keep.tile([P, PASSES, N], I32, name="wk_codes", align_bytes=64)
-        nc.vector.tensor_copy(
-            wk_codes[:].rearrange("p a (t g m) -> p a g t m", t=PACK, m=4),
-            wk_raw[:].rearrange("p a (g m t) -> p a g t m", t=PACK, m=4),
-        )
-        wv_codes = keep.tile([P, PASSES, 2 * N], U8, name="wv_codes", align_bytes=64)
-        nc.vector.tensor_copy(
-            wv_codes[:].bitcast(U16).rearrange("p a (t g m) -> p a g t m", t=PACK, m=8),
-            wv_raw[:].bitcast(U16).rearrange("p a (g m t) -> p a g t m", t=PACK, m=8),
-        )
+        wvd_rows = wvd.rearrange("(a p i) n -> a p i n", a=PASSES, i=PACK)
+        wd_raw = [keep.tile([P, PACK, N], F32, name="wd_raw0", tag="wide1", align_bytes=64)]
+        nc.sync.dma_start(wd_raw[0][:], wvd_rows[0])
 
-        picked = keep.tile([P, J], U32, name="picked", align_bytes=64)
+        picked = keep.tile([P, J], U32, name="picked", tag="wide2", align_bytes=64)
         nc.vector.tensor_copy(picked[:], tab_raw[:].bitcast(U32).indirect(offsets[:]))
         tab_codes = keep.tile([P, PASSES, 2 * J], U8, name="tab_codes", align_bytes=64)
         nc.vector.tensor_copy(
@@ -105,15 +87,39 @@ def tile_list_engram_dl_tanhLP_kernel(
             picked[:].bitcast(U16).rearrange("p (g m a) -> p g a m", a=PASSES, m=8),
         )
 
+        st_rows = st.rearrange("(p t) j -> p t j", t=PACK)
+        st_sb = [keep.tile([P, 2, J], F32, name="st_sb0", tag="pair0", align_bytes=64)]
+        nc.sync.dma_start(st_sb[0][:], st_rows[:, 0:2, :])
+        wd_raw.append(keep.tile([P, PACK, N], F32, name="wd_raw1", tag="wide2", align_bytes=64))
+        nc.sync.dma_start(wd_raw[1][:], wvd_rows[1])
+
+        wk_codes = keep.tile([P, PASSES, N], I32, name="wk_codes", align_bytes=64)
+        nc.vector.tensor_copy(
+            wk_codes[:].rearrange("p a (t g m) -> p a g t m", t=PACK, m=4),
+            wk_raw[:].rearrange("p a (g m t) -> p a g t m", t=PACK, m=4),
+        )
+        st_sb.append(keep.tile([P, 2, J], F32, name="st_sb1", tag="pair1", align_bytes=64))
+        nc.sync.dma_start(st_sb[1][:], st_rows[:, 2:4, :])
+        wv_codes = keep.tile([P, PASSES, 2 * N], U8, name="wv_codes", align_bytes=64)
+        nc.vector.tensor_copy(
+            wv_codes[:].bitcast(U16).rearrange("p a (t g m) -> p a g t m", t=PACK, m=8),
+            wv_raw[:].bitcast(U16).rearrange("p a (g m t) -> p a g t m", t=PACK, m=8),
+        )
+
         wd_codes = [keep.tile([P, N], U32, name="wd_codes%d" % a, align_bytes=64) for a in range(PASSES)]
         wd_scales = [keep.tile([P, N], U8, name="wd_scales%d" % a, align_bytes=64) for a in range(PASSES)]
         for a in range(PASSES):
-            wd_bf = keep.tile([P, PACK * N], BF16, name="wd_bf%d" % a, align_bytes=64)
+            wd_bf = keep.tile([P, PACK * N], BF16, name="wd_bf%d" % a, tag="half" if a == 0 else "wide3", align_bytes=64)
             nc.scalar.copy(
                 wd_bf[:].rearrange("p (t m i) -> p m t i", t=PACK, i=PACK),
                 wd_raw[a][:].rearrange("p i (m t) -> p m t i", t=PACK),
             )
             nc.vector.quantize_mx(out=wd_codes[a][:].bitcast(FP8X4), scales=wd_scales[a][:], in_=wd_bf[:])
+
+        r_sb = [keep.tile([P, T], F32, name="r_sb%d" % t, tag="wide%d" % t, align_bytes=64) for t in range(PACK)]
+        r_rows = rT.rearrange("(p t) c -> p t c", t=PACK)
+        for t in range(PACK):
+            nc.sync.dma_start(r_sb[t][:], r_rows[:, t, :])
 
         def product(acc, operands, h):
             count = len(operands) * PASSES
@@ -131,28 +137,36 @@ def tile_list_engram_dl_tanhLP_kernel(
                     )
                     step = step + 1
 
+        def key_operands(lo, hi):
+            return [(lambda a: wk_codes[:, a, lo:hi].bitcast(FP8X4), lambda a: planes[:, a, WK_COL + lo : WK_COL + hi])]
+
+        def value_operands(lo, hi):
+            return [
+                (
+                    lambda a: wv_codes[:, a, 2 * lo : 2 * hi].bitcast(FP4X4),
+                    lambda a: planes[:, a, WV_COL + lo : WV_COL + hi],
+                ),
+                (lambda a: wd_codes[a][:, lo:hi].bitcast(FP8X4), lambda a: wd_scales[a][:, lo:hi]),
+            ]
+
+        gate = [keep.tile([P, J], F32, name="gate%d" % t) for t in range(PACK)]
         gated = [keep.tile([P, J], F32, name="gated%d" % t) for t in range(PACK)]
         for t in range(PACK):
-            lo, hi = P * t, P * (t + 1)
-            wk_op = (lambda a: wk_codes[:, a, lo:hi].bitcast(FP8X4), lambda a: planes[:, a, WK_COL + lo : WK_COL + hi])
-            wv_op = (
-                lambda a: wv_codes[:, a, 2 * lo : 2 * hi].bitcast(FP4X4),
-                lambda a: planes[:, a, WV_COL + lo : WV_COL + hi],
-            )
-            wd_op = (lambda a: wd_codes[a][:, lo:hi].bitcast(FP8X4), lambda a: wd_scales[a][:, lo:hi])
             for h in range(J // BANK):
                 cols = slice(BANK * h, BANK * (h + 1))
                 ke = psum.tile([P, BANK], F32, name="ke")
-                product(ke, [wk_op], h)
-                ve = psum.tile([P, BANK], F32, name="ve")
-                product(ve, [wv_op, wd_op], h)
+                product(ke, key_operands(P * t, P * (t + 1)), h)
                 score = work.tile([P, BANK], F32, name="score")
                 nc.vector.tensor_tensor(score[:], ke[:], st_sb[t // 2][:, t % 2, cols], MULT)
-                gate = work.tile([P, BANK], F32, name="gate")
-                nc.scalar.activation(gate[:], score[:], TANH)
-                nc.vector.tensor_tensor(gated[t][:, cols], ve[:], gate[:], MULT)
+                nc.scalar.activation(gate[t][:, cols], score[:], TANH)
+        for t in range(PACK):
+            for h in range(J // BANK):
+                cols = slice(BANK * h, BANK * (h + 1))
+                ve = psum.tile([P, BANK], F32, name="ve")
+                product(ve, value_operands(P * t, P * (t + 1)), h)
+                nc.vector.tensor_tensor(gated[t][:, cols], ve[:], gate[t][:, cols], MULT)
 
-        y = [keep.tile([P, 2, J], F32, name="y%d" % u, tag="pair%d" % u) for u in range(2)]
+        y = [keep.tile([P, 2, J], F32, name="y%d" % u, tag="pair%d" % u, align_bytes=64) for u in range(2)]
         y_bf = [keep.tile([P, w, PACK], BF16, name="y_bf%d" % c, align_bytes=64) for c, w in enumerate(CHUNKS)]
         y_codes = keep.tile([P, J], U32, name="y_codes", align_bytes=64)
         y_scales = keep.tile([P, J], U8, name="y_scales", align_bytes=64)

@@ -41,7 +41,7 @@ def tile_list_engram_dl_tanhLP_kernel(
         tab_sc = keep.tile([P, T], U8, name="tab_sc", align_bytes=64)
         w_sc = keep.tile([P, 2 * N], U8, name="w_sc", align_bytes=64)
         planes = keep.tile([P, PASSES, PLANE], U8, name="planes", align_bytes=64)
-        tab_raw = keep.tile([P, T], I32, name="tab_raw", tag="pair0", align_bytes=64)
+        tab_raw = keep.tile([P, T], I32, name="tab_raw", tag="wide2", align_bytes=64)
         wk_raw = keep.tile([P, PASSES, N], I32, name="wk_raw", tag="pair1", align_bytes=64)
         wv_raw = keep.tile([P, PASSES, 2 * N], U8, name="wv_raw", tag="wide0", align_bytes=64)
 
@@ -67,19 +67,24 @@ def tile_list_engram_dl_tanhLP_kernel(
         picked_sc = keep.tile([P, J], U8, name="picked_sc", tag="wide1", align_bytes=64)
         nc.vector.tensor_copy(picked_sc[:], tab_sc[:].indirect(offsets[:]))
         nc.vector.tensor_copy(all_sc[:, 0:J].bitcast(I32), picked_sc[:].bitcast(I32))
-        for a in range(PASSES):
-            for r in range(4):
-                queue = nc.gpsimd if 4 * a + r < 3 else nc.sync
-                queue.dma_start(
-                    planes[r:P:32, a, :].bitcast(I32),
-                    all_sc[ROWS * a + r : ROWS * (a + 1) : 4, :].bitcast(I32),
-                )
+        moves = [(a, r) for a in range(PASSES) for r in range(4)]
+
+        def move_rows(a, r):
+            nc.sync.dma_start(
+                planes[r:P:32, a, :].bitcast(I32),
+                all_sc[ROWS * a + r : ROWS * (a + 1) : 4, :].bitcast(I32),
+            )
+
+        for a, r in moves[:5]:
+            move_rows(a, r)
 
         wvd_rows = wvd.rearrange("(a p i) n -> a p i n", a=PASSES, i=PACK)
         wd_raw = [keep.tile([P, PACK, N], F32, name="wd_raw0", tag="wide1", align_bytes=64)]
         nc.sync.dma_start(wd_raw[0][:], wvd_rows[0])
+        for a, r in moves[5:]:
+            move_rows(a, r)
 
-        picked = keep.tile([P, J], U32, name="picked", tag="wide2", align_bytes=64)
+        picked = keep.tile([P, J], U32, name="picked", tag="pair0", align_bytes=64)
         nc.vector.tensor_copy(picked[:], tab_raw[:].bitcast(U32).indirect(offsets[:]))
         tab_codes = keep.tile([P, PASSES, 2 * J], U8, name="tab_codes", align_bytes=64)
         nc.vector.tensor_copy(
@@ -88,10 +93,11 @@ def tile_list_engram_dl_tanhLP_kernel(
         )
 
         st_rows = st.rearrange("(p t) j -> p t j", t=PACK)
-        st_sb = [keep.tile([P, 2, J], F32, name="st_sb0", tag="pair0", align_bytes=64)]
-        nc.sync.dma_start(st_sb[0][:], st_rows[:, 0:2, :])
         wd_raw.append(keep.tile([P, PACK, N], F32, name="wd_raw1", tag="wide2", align_bytes=64))
         nc.sync.dma_start(wd_raw[1][:], wvd_rows[1])
+        st_sb = [keep.tile([P, 2, J], F32, name="st_sb0", tag="pair0", align_bytes=64)]
+        for t in range(2):
+            nc.sync.dma_start(st_sb[0][:, t, :], st_rows[:, t, :])
 
         wk_codes = keep.tile([P, PASSES, N], I32, name="wk_codes", align_bytes=64)
         nc.vector.tensor_copy(
@@ -99,7 +105,8 @@ def tile_list_engram_dl_tanhLP_kernel(
             wk_raw[:].rearrange("p a (g m t) -> p a g t m", t=PACK, m=4),
         )
         st_sb.append(keep.tile([P, 2, J], F32, name="st_sb1", tag="pair1", align_bytes=64))
-        nc.sync.dma_start(st_sb[1][:], st_rows[:, 2:4, :])
+        for t in range(2):
+            nc.sync.dma_start(st_sb[1][:, t, :], st_rows[:, 2 + t, :])
         wv_codes = keep.tile([P, PASSES, 2 * N], U8, name="wv_codes", align_bytes=64)
         nc.vector.tensor_copy(
             wv_codes[:].bitcast(U16).rearrange("p a (t g m) -> p a g t m", t=PACK, m=8),

@@ -22,7 +22,8 @@ PACK = 4
 PASSES = K // (P * PACK)
 BANK = 512
 ROWS = 16
-CHUNKS = [256, 256, 256, 256]
+CHUNKS = [128, 256, 256, 256, 128]
+STORE_CUT = 640
 WK_COL = J
 WV_COL = J + N
 PLANE = J + 2 * N
@@ -46,17 +47,17 @@ def tile_list_engram_dl_tanhLP_kernel(
         wv_raw = keep.tile([P, PASSES, 2 * N], U8, name="wv_raw", tag="wide0", align_bytes=64)
 
         live = PASSES * ROWS
-        nc.sync.dma_start(offsets[:], offs)
-        nc.sync.dma_start(tab_sc[0:live, :].bitcast(I32), tab_scales.rearrange("a q t -> (a q) t").bitcast(I32))
         nc.sync.dma_start(w_sc[0:live, 0:N].bitcast(I32), wk_scales.rearrange("a q n -> (a q) n").bitcast(I32))
         nc.sync.dma_start(w_sc[0:live, N : 2 * N].bitcast(I32), wv4_scales.rearrange("a q n -> (a q) n").bitcast(I32))
+        nc.sync.dma_start(tab_sc[0:live, :].bitcast(I32), tab_scales.rearrange("a q t -> (a q) t").bitcast(I32))
+        nc.sync.dma_start(offsets[:], offs)
         nc.sync.dma_start(tab_raw[:], tab_words[0].rearrange("p t b -> p (t b)").bitcast(I32))
         nc.sync.dma_start(wk_raw[:], wk_words.rearrange("a p n i -> p a (n i)").bitcast(I32))
         nc.sync.dma_start(wv_raw[:].bitcast(I32), wv4_words.rearrange("a p b -> p a b").bitcast(I32))
 
         for rows in (slice(32, 64), slice(64, P)):
-            nc.vector.memset(tab_sc[rows, :].bitcast(I32), 0)
             nc.vector.memset(w_sc[rows, :].bitcast(I32), 0)
+            nc.vector.memset(tab_sc[rows, :].bitcast(I32), 0)
         nc.gpsimd.memset(planes[:].rearrange("p a c -> p (a c)").bitcast(I32), 0)
 
         all_sc = keep.tile([P, PLANE], U8, name="all_sc", align_bytes=64)
@@ -75,13 +76,13 @@ def tile_list_engram_dl_tanhLP_kernel(
                 all_sc[ROWS * a + r : ROWS * (a + 1) : 4, :].bitcast(I32),
             )
 
-        for a, r in moves[:5]:
+        for a, r in moves[:2]:
             move_rows(a, r)
 
         wvd_rows = wvd.rearrange("(a p i) n -> a p i n", a=PASSES, i=PACK)
         wd_raw = [keep.tile([P, PACK, N], F32, name="wd_raw0", tag="wide1", align_bytes=64)]
         nc.sync.dma_start(wd_raw[0][:], wvd_rows[0])
-        for a, r in moves[5:]:
+        for a, r in moves[2:]:
             move_rows(a, r)
 
         picked = keep.tile([P, J], U32, name="picked", tag="pair0", align_bytes=64)
@@ -166,47 +167,58 @@ def tile_list_engram_dl_tanhLP_kernel(
                 score = work.tile([P, BANK], F32, name="score")
                 nc.vector.tensor_tensor(score[:], ke[:], st_sb[t // 2][:, t % 2, cols], MULT)
                 nc.scalar.activation(gate[t][:, cols], score[:], TANH)
-        for t in range(PACK):
+
+        y = [keep.tile([P, 2, J], F32, name="y%d" % u, tag="pair%d" % u, align_bytes=64) for u in range(2)]
+
+        def gate_values(t):
             for h in range(J // BANK):
                 cols = slice(BANK * h, BANK * (h + 1))
                 ve = psum.tile([P, BANK], F32, name="ve")
                 product(ve, value_operands(P * t, P * (t + 1)), h)
                 nc.vector.tensor_tensor(gated[t][:, cols], ve[:], gate[t][:, cols], MULT)
 
-        y = [keep.tile([P, 2, J], F32, name="y%d" % u, tag="pair%d" % u, align_bytes=64) for u in range(2)]
+        def add_record(t, cols):
+            picks = offsets[:, cols.start // 16 : cols.stop // 16]
+            nc.vector.tensor_tensor(y[t // 2][:, t % 2, cols], r_sb[t][:].indirect(picks), gated[t][:, cols], ADD)
+
         y_bf = [keep.tile([P, w, PACK], BF16, name="y_bf%d" % c, align_bytes=64) for c, w in enumerate(CHUNKS)]
         y_codes = keep.tile([P, J], U32, name="y_codes", align_bytes=64)
         y_scales = keep.tile([P, J], U8, name="y_scales", align_bytes=64)
         out_rows = out_0.rearrange("(p t) j -> p t j", t=PACK)
         out_words = out_1[0].rearrange("p j i -> p (j i)").bitcast(I32)
-        starts = [sum(CHUNKS[:c]) for c in range(len(CHUNKS))]
+        pieces = [slice(sum(CHUNKS[:c]), sum(CHUNKS[: c + 1])) for c in range(len(CHUNKS))]
+        stores = {STORE_CUT: slice(0, STORE_CUT), J: slice(STORE_CUT, J)}
 
         def round_pair(u, c):
-            cols = slice(starts[c], starts[c] + CHUNKS[c])
-            nc.scalar.copy(y_bf[c][:, :, 2 * u : 2 * u + 2], y[u][:, :, cols].rearrange("p t j -> p j t"))
+            nc.scalar.copy(y_bf[c][:, :, 2 * u : 2 * u + 2], y[u][:, :, pieces[c]].rearrange("p t j -> p j t"))
 
-        for t in range(PACK - 1):
-            nc.vector.tensor_tensor(y[t // 2][:, t % 2, :], r_sb[t][:].indirect(offsets[:]), gated[t][:], ADD)
-            if t == 1:
-                nc.sync.dma_start(out_rows[:, 0:2, :], y[0][:])
-                for c in range(len(CHUNKS)):
-                    round_pair(0, c)
+        whole = slice(0, J)
+        gate_values(0)
+        gate_values(1)
+        add_record(0, whole)
+        gate_values(2)
+        gate_values(3)
+        add_record(1, whole)
+        nc.sync.dma_start(out_rows[:, 0:2, :], y[0][:])
+        for c in range(len(CHUNKS)):
+            round_pair(0, c)
+        add_record(2, whole)
         nc.sync.dma_start(out_rows[:, 2, :], y[1][:, 0, :])
         last = PACK - 1
-        for c in range(len(CHUNKS) + 1):
-            if c < len(CHUNKS):
-                cols = slice(starts[c], starts[c] + CHUNKS[c])
-                picks = offsets[:, cols.start // 16 : cols.stop // 16]
-                nc.vector.tensor_tensor(y[1][:, 1, cols], r_sb[last][:].indirect(picks), gated[last][:, cols], ADD)
-                nc.sync.dma_start(out_rows[:, last, cols], y[1][:, 1, cols])
-                round_pair(1, c)
-            if c > 0:
-                cols = slice(starts[c - 1], starts[c - 1] + CHUNKS[c - 1])
-                nc.vector.quantize_mx(
-                    out=y_codes[:, cols].bitcast(FP8X4),
-                    scales=y_scales[:, cols],
-                    in_=y_bf[c - 1][:].rearrange("p j t -> p (j t)"),
-                )
-                nc.sync.dma_start(out_words[:, cols], y_codes[:, cols].bitcast(I32))
+        for c, cols in enumerate(pieces):
+            add_record(last, cols)
+            if cols.stop in stores:
+                part = stores[cols.stop]
+                nc.sync.dma_start(out_rows[:, last, part], y[1][:, 1, part])
+            round_pair(1, c)
+        for c, cols in enumerate(pieces):
+            nc.vector.quantize_mx(
+                out=y_codes[:, cols].bitcast(FP8X4),
+                scales=y_scales[:, cols],
+                in_=y_bf[c][:].rearrange("p j t -> p (j t)"),
+            )
+            if cols.stop in stores:
+                part = stores[cols.stop]
+                nc.sync.dma_start(out_words[:, part], y_codes[:, part].bitcast(I32))
         for q in range(4):
             nc.scalar.dma_start(out_2[0, 4 * q : 4 * q + 4, :].bitcast(I32), y_scales[32 * q : 32 * q + 4, :].bitcast(I32))

@@ -42,18 +42,21 @@ def tile_list_engram_dl_tanhLP_kernel(
         tab_sc = keep.tile([P, T], U8, name="tab_sc", align_bytes=64)
         w_sc = keep.tile([P, 2 * N], U8, name="w_sc", align_bytes=64)
         planes = keep.tile([P, PASSES, PLANE], U8, name="planes", align_bytes=64)
-        tab_raw = keep.tile([P, T], I32, name="tab_raw", tag="wide2", align_bytes=64)
+        tab_raw = keep.tile([P, T], I32, name="tab_raw", align_bytes=64)
         wk_raw = keep.tile([P, PASSES, N], I32, name="wk_raw", tag="pair1", align_bytes=64)
         wv_raw = keep.tile([P, PASSES, 2 * N], U8, name="wv_raw", tag="wide0", align_bytes=64)
 
         live = PASSES * ROWS
-        nc.sync.dma_start(w_sc[0:live, 0:N].bitcast(I32), wk_scales.rearrange("a q n -> (a q) n").bitcast(I32))
-        nc.sync.dma_start(w_sc[0:live, N : 2 * N].bitcast(I32), wv4_scales.rearrange("a q n -> (a q) n").bitcast(I32))
-        nc.sync.dma_start(tab_sc[0:live, :].bitcast(I32), tab_scales.rearrange("a q t -> (a q) t").bitcast(I32))
+        nc.scalar.dma_start(w_sc[0:live, 0:N].bitcast(I32), wk_scales.rearrange("a q n -> (a q) n").bitcast(I32))
+        nc.scalar.dma_start(w_sc[0:live, N : 2 * N].bitcast(I32), wv4_scales.rearrange("a q n -> (a q) n").bitcast(I32))
         nc.sync.dma_start(offsets[:], offs)
+        nc.sync.dma_start(tab_sc[0:live, :].bitcast(I32), tab_scales.rearrange("a q t -> (a q) t").bitcast(I32))
         nc.sync.dma_start(tab_raw[:], tab_words[0].rearrange("p t b -> p (t b)").bitcast(I32))
         nc.sync.dma_start(wk_raw[:], wk_words.rearrange("a p n i -> p a (n i)").bitcast(I32))
         nc.sync.dma_start(wv_raw[:].bitcast(I32), wv4_words.rearrange("a p b -> p a b").bitcast(I32))
+        wvd_rows = wvd.rearrange("(a p i) n -> a p i n", a=PASSES, i=PACK)
+        wd_raw = [keep.tile([P, PACK, N], F32, name="wd_raw0", tag="wide1", align_bytes=64)]
+        nc.sync.dma_start(wd_raw[0][:], wvd_rows[0])
 
         for rows in (slice(32, 64), slice(64, P)):
             nc.vector.memset(w_sc[rows, :].bitcast(I32), 0)
@@ -65,7 +68,7 @@ def tile_list_engram_dl_tanhLP_kernel(
             all_sc[:, J:PLANE].rearrange("p (w t m) -> p w t m", w=2, t=PACK),
             w_sc[:].rearrange("p (w m t) -> p w t m", w=2, t=PACK),
         )
-        picked_sc = keep.tile([P, J], U8, name="picked_sc", tag="wide1", align_bytes=64)
+        picked_sc = keep.tile([P, J], U8, name="picked_sc", tag="wide2", align_bytes=64)
         nc.vector.tensor_copy(picked_sc[:], tab_sc[:].indirect(offsets[:]))
         nc.vector.tensor_copy(all_sc[:, 0:J].bitcast(I32), picked_sc[:].bitcast(I32))
         moves = [(a, r) for a in range(PASSES) for r in range(4)]
@@ -76,13 +79,12 @@ def tile_list_engram_dl_tanhLP_kernel(
                 all_sc[ROWS * a + r : ROWS * (a + 1) : 4, :].bitcast(I32),
             )
 
-        for a, r in moves[:2]:
+        for a, r in moves[:3]:
             move_rows(a, r)
 
-        wvd_rows = wvd.rearrange("(a p i) n -> a p i n", a=PASSES, i=PACK)
-        wd_raw = [keep.tile([P, PACK, N], F32, name="wd_raw0", tag="wide1", align_bytes=64)]
-        nc.sync.dma_start(wd_raw[0][:], wvd_rows[0])
-        for a, r in moves[2:]:
+        wd_raw.append(keep.tile([P, PACK, N], F32, name="wd_raw1", tag="wide2", align_bytes=64))
+        nc.sync.dma_start(wd_raw[1][:], wvd_rows[1])
+        for a, r in moves[3:]:
             move_rows(a, r)
 
         picked = keep.tile([P, J], U32, name="picked", tag="pair0", align_bytes=64)
@@ -94,11 +96,8 @@ def tile_list_engram_dl_tanhLP_kernel(
         )
 
         st_rows = st.rearrange("(p t) j -> p t j", t=PACK)
-        wd_raw.append(keep.tile([P, PACK, N], F32, name="wd_raw1", tag="wide2", align_bytes=64))
-        nc.sync.dma_start(wd_raw[1][:], wvd_rows[1])
         st_sb = [keep.tile([P, 2, J], F32, name="st_sb0", tag="pair0", align_bytes=64)]
-        for t in range(2):
-            nc.sync.dma_start(st_sb[0][:, t, :], st_rows[:, t, :])
+        nc.sync.dma_start(st_sb[0][:], st_rows[:, 0:2, :])
 
         wk_codes = keep.tile([P, PASSES, N], I32, name="wk_codes", align_bytes=64)
         nc.vector.tensor_copy(
@@ -106,8 +105,7 @@ def tile_list_engram_dl_tanhLP_kernel(
             wk_raw[:].rearrange("p a (g m t) -> p a g t m", t=PACK, m=4),
         )
         st_sb.append(keep.tile([P, 2, J], F32, name="st_sb1", tag="pair1", align_bytes=64))
-        for t in range(2):
-            nc.sync.dma_start(st_sb[1][:, t, :], st_rows[:, 2 + t, :])
+        nc.sync.dma_start(st_sb[1][:], st_rows[:, 2:4, :])
         wv_codes = keep.tile([P, PASSES, 2 * N], U8, name="wv_codes", align_bytes=64)
         nc.vector.tensor_copy(
             wv_codes[:].bitcast(U16).rearrange("p a (t g m) -> p a g t m", t=PACK, m=8),

@@ -27,6 +27,7 @@ STORE_CUT = 640
 WK_COL = J
 WV_COL = J + N
 PLANE = J + 2 * N
+PICKED_AT = [7 * 1024, 8 * 1024]
 
 
 def tile_list_engram_dl_tanhLP_kernel(
@@ -35,87 +36,81 @@ def tile_list_engram_dl_tanhLP_kernel(
     nc = tc.nc
     with ExitStack() as ctx:
         keep = ctx.enter_context(tc.tile_pool(name="keep", bufs=1))
+        laid = ctx.enter_context(tc.tile_pool(name="laid", bufs=1))
         work = ctx.enter_context(tc.tile_pool(name="work", bufs=4))
-        psum = ctx.enter_context(tc.psum_pool(name="psum", bufs=4))
+        psum = ctx.enter_context(tc.psum_pool(name="psum", bufs=8))
 
+        halves = range(J // BANK)
+        live = PASSES * ROWS
         offsets = keep.tile([P, J // 16], U16, name="offsets")
-        tab_sc = keep.tile([P, T], U8, name="tab_sc", align_bytes=64)
+        tab_sc = keep.tile([P, T], U8, name="tab_sc", tag="pair1", align_bytes=64)
         w_sc = keep.tile([P, 2 * N], U8, name="w_sc", align_bytes=64)
         planes = keep.tile([P, PASSES, PLANE], U8, name="planes", align_bytes=64)
         tab_raw = keep.tile([P, T], I32, name="tab_raw", align_bytes=64)
-        wk_raw = keep.tile([P, PASSES, N], I32, name="wk_raw", tag="pair1", align_bytes=64)
-        wv_raw = keep.tile([P, PASSES, 2 * N], U8, name="wv_raw", tag="wide0", align_bytes=64)
+        wk_raw = keep.tile([P, PASSES, N], I32, name="wk_raw", align_bytes=64)
 
-        live = PASSES * ROWS
-        nc.scalar.dma_start(w_sc[0:live, 0:N].bitcast(I32), wk_scales.rearrange("a q n -> (a q) n").bitcast(I32))
-        nc.scalar.dma_start(w_sc[0:live, N : 2 * N].bitcast(I32), wv4_scales.rearrange("a q n -> (a q) n").bitcast(I32))
+        nc.scalar.dma_start(w_sc[0:live, 0:N].bitcast(I32), wk_scales.rearrange("a q n -> q a n").bitcast(I32))
+        nc.scalar.dma_start(w_sc[0:live, N : 2 * N].bitcast(I32), wv4_scales.rearrange("a q n -> q a n").bitcast(I32))
         nc.sync.dma_start(offsets[:], offs)
-        nc.sync.dma_start(tab_sc[0:live, :].bitcast(I32), tab_scales.rearrange("a q t -> (a q) t").bitcast(I32))
-        nc.sync.dma_start(tab_raw[:], tab_words[0].rearrange("p t b -> p (t b)").bitcast(I32))
+        nc.sync.dma_start(tab_sc[0:live, :].bitcast(I32), tab_scales.rearrange("a q t -> q a t").bitcast(I32))
         nc.sync.dma_start(wk_raw[:], wk_words.rearrange("a p n i -> p a (n i)").bitcast(I32))
-        nc.sync.dma_start(wv_raw[:].bitcast(I32), wv4_words.rearrange("a p b -> p a b").bitcast(I32))
-        wvd_rows = wvd.rearrange("(a p i) n -> a p i n", a=PASSES, i=PACK)
-        wd_raw = [keep.tile([P, PACK, N], F32, name="wd_raw0", tag="wide1", align_bytes=64)]
-        nc.sync.dma_start(wd_raw[0][:], wvd_rows[0])
+        nc.sync.dma_start(tab_raw[:], tab_words[0].rearrange("p t b -> p (t b)").bitcast(I32))
 
         for rows in (slice(32, 64), slice(64, P)):
             nc.vector.memset(w_sc[rows, :].bitcast(I32), 0)
             nc.vector.memset(tab_sc[rows, :].bitcast(I32), 0)
         nc.gpsimd.memset(planes[:].rearrange("p a c -> p (a c)").bitcast(I32), 0)
 
-        all_sc = keep.tile([P, PLANE], U8, name="all_sc", align_bytes=64)
+        all_sc = keep.tile([P, PLANE], U8, name="all_sc", tag="wide2", align_bytes=64)
         nc.vector.tensor_copy(
             all_sc[:, J:PLANE].rearrange("p (w t m) -> p w t m", w=2, t=PACK),
             w_sc[:].rearrange("p (w m t) -> p w t m", w=2, t=PACK),
         )
-        picked_sc = keep.tile([P, J], U8, name="picked_sc", tag="wide2", align_bytes=64)
+        picked_sc = keep.tile([P, J], U8, name="picked_sc", tag="wide0", align_bytes=64)
         nc.vector.tensor_copy(picked_sc[:], tab_sc[:].indirect(offsets[:]))
         nc.vector.tensor_copy(all_sc[:, 0:J].bitcast(I32), picked_sc[:].bitcast(I32))
-        moves = [(a, r) for a in range(PASSES) for r in range(4)]
+        wv_raw = keep.tile([P, PASSES, 2 * N], U8, name="wv_raw", tag="pair1", align_bytes=64)
+        nc.sync.dma_start(wv_raw[:].bitcast(I32), wv4_words.rearrange("a p b -> p a b").bitcast(I32))
+        for q in (0, 2, 1, 3):
+            nc.sync.dma_start(planes[32 * q : 32 * q + 4, :, :].bitcast(I32), all_sc[8 * q : 8 * q + 8, :].bitcast(I32))
 
-        def move_rows(a, r):
-            nc.sync.dma_start(
-                planes[r:P:32, a, :].bitcast(I32),
-                all_sc[ROWS * a + r : ROWS * (a + 1) : 4, :].bitcast(I32),
-            )
-
-        for a, r in moves[:3]:
-            move_rows(a, r)
-
-        wd_raw.append(keep.tile([P, PACK, N], F32, name="wd_raw1", tag="wide2", align_bytes=64))
-        nc.sync.dma_start(wd_raw[1][:], wvd_rows[1])
-        for a, r in moves[3:]:
-            move_rows(a, r)
-
-        picked = keep.tile([P, J], U32, name="picked", tag="pair0", align_bytes=64)
-        nc.vector.tensor_copy(picked[:], tab_raw[:].bitcast(U32).indirect(offsets[:]))
-        tab_codes = keep.tile([P, PASSES, 2 * J], U8, name="tab_codes", align_bytes=64)
-        nc.vector.tensor_copy(
-            tab_codes[:].bitcast(U16).rearrange("p a (g m) -> p g a m", m=8),
-            picked[:].bitcast(U16).rearrange("p (g m a) -> p g a m", a=PASSES, m=8),
-        )
-
-        st_rows = st.rearrange("(p t) j -> p t j", t=PACK)
-        st_sb = [keep.tile([P, 2, J], F32, name="st_sb0", tag="pair0", align_bytes=64)]
-        nc.sync.dma_start(st_sb[0][:], st_rows[:, 0:2, :])
+        wvd_rows = wvd.rearrange("(a p i) n -> a p i n", a=PASSES, i=PACK)
+        wd_raw = [keep.tile([P, PACK, N], F32, name="wd_raw%d" % a, tag="wide%d" % (2 * a), align_bytes=64) for a in range(PASSES)]
+        for a in range(PASSES):
+            nc.sync.dma_start(wd_raw[a][:], wvd_rows[a])
 
         wk_codes = keep.tile([P, PASSES, N], I32, name="wk_codes", align_bytes=64)
         nc.vector.tensor_copy(
             wk_codes[:].rearrange("p a (t g m) -> p a g t m", t=PACK, m=4),
             wk_raw[:].rearrange("p a (g m t) -> p a g t m", t=PACK, m=4),
         )
-        st_sb.append(keep.tile([P, 2, J], F32, name="st_sb1", tag="pair1", align_bytes=64))
-        nc.sync.dma_start(st_sb[1][:], st_rows[:, 2:4, :])
+
+        tab_codes = []
+        for h in halves:
+            picked = laid.tile([P, BANK], U32, name="picked%d" % h, offset=PICKED_AT[h], align_bytes=64)
+            picks = offsets[:, BANK // 16 * h : BANK // 16 * (h + 1)]
+            nc.vector.tensor_copy(picked[:], tab_raw[:].bitcast(U32).indirect(picks))
+            tab_codes.append(keep.tile([P, PASSES, 2 * BANK], U8, name="tab_codes%d" % h, align_bytes=64))
+            nc.vector.tensor_copy(
+                tab_codes[h][:].bitcast(U16).rearrange("p a (g m) -> p g a m", m=8),
+                picked[:].bitcast(U16).rearrange("p (g m a) -> p g a m", a=PASSES, m=8),
+            )
+
+        st_rows = st.rearrange("(p t) j -> p t j", t=PACK)
+        st_sb = [laid.tile([P, 2, J], F32, name="st_sb0", offset=0, align_bytes=64)]
+        nc.sync.dma_start(st_sb[0][:], st_rows[:, 0:2, :])
         wv_codes = keep.tile([P, PASSES, 2 * N], U8, name="wv_codes", align_bytes=64)
         nc.vector.tensor_copy(
             wv_codes[:].bitcast(U16).rearrange("p a (t g m) -> p a g t m", t=PACK, m=8),
             wv_raw[:].bitcast(U16).rearrange("p a (g m t) -> p a g t m", t=PACK, m=8),
         )
+        st_sb.append(keep.tile([P, 2, J], F32, name="st_sb1", tag="pair1", align_bytes=64))
+        nc.sync.dma_start(st_sb[1][:], st_rows[:, 2:4, :])
 
         wd_codes = [keep.tile([P, N], U32, name="wd_codes%d" % a, align_bytes=64) for a in range(PASSES)]
         wd_scales = [keep.tile([P, N], U8, name="wd_scales%d" % a, align_bytes=64) for a in range(PASSES)]
         for a in range(PASSES):
-            wd_bf = keep.tile([P, PACK * N], BF16, name="wd_bf%d" % a, tag="half" if a == 0 else "wide3", align_bytes=64)
+            wd_bf = keep.tile([P, PACK * N], BF16, name="wd_bf%d" % a, tag="wide%d" % (2 * a + 1), align_bytes=64)
             nc.scalar.copy(
                 wd_bf[:].rearrange("p (t m i) -> p m t i", t=PACK, i=PACK),
                 wd_raw[a][:].rearrange("p i (m t) -> p m t i", t=PACK),
@@ -127,53 +122,79 @@ def tile_list_engram_dl_tanhLP_kernel(
         for t in range(PACK):
             nc.sync.dma_start(r_sb[t][:], r_rows[:, t, :])
 
-        def product(acc, operands, h):
-            count = len(operands) * PASSES
-            step = 0
-            for codes, scales in operands:
-                for a in range(PASSES):
-                    nc.tensor.matmul_mx(
-                        out=acc[:],
-                        lhsT=codes(a),
-                        lhsT_scale=scales(a),
-                        rhs=tab_codes[:, a, 2 * BANK * h : 2 * BANK * (h + 1)].bitcast(FP4X4),
-                        rhs_scale=planes[:, a, BANK * h : BANK * (h + 1)],
-                        start=(step == 0),
-                        stop=(step == count - 1),
-                    )
-                    step = step + 1
-
-        def key_operands(lo, hi):
-            return [(lambda a: wk_codes[:, a, lo:hi].bitcast(FP8X4), lambda a: planes[:, a, WK_COL + lo : WK_COL + hi])]
-
-        def value_operands(lo, hi):
-            return [
-                (
-                    lambda a: wv_codes[:, a, 2 * lo : 2 * hi].bitcast(FP4X4),
-                    lambda a: planes[:, a, WV_COL + lo : WV_COL + hi],
-                ),
-                (lambda a: wd_codes[a][:, lo:hi].bitcast(FP8X4), lambda a: wd_scales[a][:, lo:hi]),
-            ]
+        def one_pass(acc, codes, scales, a, h, start, stop):
+            nc.tensor.matmul_mx(
+                out=acc[:],
+                lhsT=codes,
+                lhsT_scale=scales,
+                rhs=tab_codes[h][:, a, :].bitcast(FP4X4),
+                rhs_scale=planes[:, a, BANK * h : BANK * (h + 1)],
+                start=start,
+                stop=stop,
+            )
 
         gate = [keep.tile([P, J], F32, name="gate%d" % t) for t in range(PACK)]
         gated = [keep.tile([P, J], F32, name="gated%d" % t) for t in range(PACK)]
-        for t in range(PACK):
-            for h in range(J // BANK):
+        y = [
+            laid.tile([P, 2, J], F32, name="y0", offset=0, align_bytes=64),
+            keep.tile([P, 2, J], F32, name="y1", tag="pair1", align_bytes=64),
+        ]
+        ke = {}
+        ve = {}
+
+        def key(t, h):
+            lo, hi = P * t, P * (t + 1)
+            ke[t, h] = psum.tile([P, BANK], F32, name="acc")
+            for a in range(PASSES):
+                codes = wk_codes[:, a, lo:hi].bitcast(FP8X4)
+                one_pass(ke[t, h], codes, planes[:, a, WK_COL + lo : WK_COL + hi], a, h, a == 0, a == PASSES - 1)
+
+        def base_values(t):
+            lo, hi = P * t, P * (t + 1)
+            for h in halves:
+                ve[t, h] = psum.tile([P, BANK], F32, name="acc")
+                for a in range(PASSES):
+                    codes = wv_codes[:, a, 2 * lo : 2 * hi].bitcast(FP4X4)
+                    one_pass(ve[t, h], codes, planes[:, a, WV_COL + lo : WV_COL + hi], a, h, a == 0, False)
+
+        def change_values(t, a):
+            lo, hi = P * t, P * (t + 1)
+            for h in halves:
+                codes = wd_codes[a][:, lo:hi].bitcast(FP8X4)
+                one_pass(ve[t, h], codes, wd_scales[a][:, lo:hi], a, h, False, a == PASSES - 1)
+
+        def make_gate(t):
+            for h in halves:
                 cols = slice(BANK * h, BANK * (h + 1))
-                ke = psum.tile([P, BANK], F32, name="ke")
-                product(ke, key_operands(P * t, P * (t + 1)), h)
                 score = work.tile([P, BANK], F32, name="score")
-                nc.vector.tensor_tensor(score[:], ke[:], st_sb[t // 2][:, t % 2, cols], MULT)
+                nc.vector.tensor_tensor(score[:], ke[t, h][:], st_sb[t // 2][:, t % 2, cols], MULT)
                 nc.scalar.activation(gate[t][:, cols], score[:], TANH)
 
-        y = [keep.tile([P, 2, J], F32, name="y%d" % u, tag="pair%d" % u, align_bytes=64) for u in range(2)]
-
         def gate_values(t):
-            for h in range(J // BANK):
+            for h in halves:
                 cols = slice(BANK * h, BANK * (h + 1))
-                ve = psum.tile([P, BANK], F32, name="ve")
-                product(ve, value_operands(P * t, P * (t + 1)), h)
-                nc.vector.tensor_tensor(gated[t][:, cols], ve[:], gate[t][:, cols], MULT)
+                nc.vector.tensor_tensor(gated[t][:, cols], ve[t, h][:], gate[t][:, cols], MULT)
+
+        for h in halves:
+            for t in (0, 1):
+                key(t, h)
+        for t in (0, 1):
+            base_values(t)
+        for t in (0, 1):
+            change_values(t, 0)
+        for t in (0, 1):
+            make_gate(t)
+            for h in halves:
+                key(t + 2, h)
+        for t in (0, 1):
+            change_values(t, 1)
+        for t in (2, 3):
+            make_gate(t)
+
+        def values(t):
+            base_values(t)
+            for a in range(PASSES):
+                change_values(t, a)
 
         def add_record(t, cols):
             picks = offsets[:, cols.start // 16 : cols.stop // 16]
@@ -191,7 +212,9 @@ def tile_list_engram_dl_tanhLP_kernel(
             nc.scalar.copy(y_bf[c][:, :, 2 * u : 2 * u + 2], y[u][:, :, pieces[c]].rearrange("p t j -> p j t"))
 
         whole = slice(0, J)
+        values(2)
         gate_values(0)
+        values(3)
         gate_values(1)
         add_record(0, whole)
         gate_values(2)

@@ -28,6 +28,7 @@ WK_COL = J
 WV_COL = J + N
 PLANE = J + 2 * N
 PICKED_AT = [7 * 1024, 8 * 1024]
+SEAM = 28 * 1024
 
 
 def tile_list_engram_dl_tanhLP_kernel(
@@ -61,12 +62,12 @@ def tile_list_engram_dl_tanhLP_kernel(
             nc.vector.memset(tab_sc[rows, :].bitcast(I32), 0)
         nc.gpsimd.memset(planes[:].rearrange("p a c -> p (a c)").bitcast(I32), 0)
 
-        all_sc = keep.tile([P, PLANE], U8, name="all_sc", tag="wide2", align_bytes=64)
+        all_sc = keep.tile([P, PLANE], U8, name="all_sc", align_bytes=64)
         nc.vector.tensor_copy(
             all_sc[:, J:PLANE].rearrange("p (w t m) -> p w t m", w=2, t=PACK),
             w_sc[:].rearrange("p (w m t) -> p w t m", w=2, t=PACK),
         )
-        picked_sc = keep.tile([P, J], U8, name="picked_sc", tag="wide0", align_bytes=64)
+        picked_sc = laid.tile([P, J], U8, name="picked_sc", offset=SEAM - J // 2, align_bytes=64)
         nc.vector.tensor_copy(picked_sc[:], tab_sc[:].indirect(offsets[:]))
         nc.vector.tensor_copy(all_sc[:, 0:J].bitcast(I32), picked_sc[:].bitcast(I32))
         wv_raw = keep.tile([P, PASSES, 2 * N], U8, name="wv_raw", tag="pair1", align_bytes=64)
@@ -75,7 +76,10 @@ def tile_list_engram_dl_tanhLP_kernel(
             nc.sync.dma_start(planes[32 * q : 32 * q + 4, :, :].bitcast(I32), all_sc[8 * q : 8 * q + 8, :].bitcast(I32))
 
         wvd_rows = wvd.rearrange("(a p i) n -> a p i n", a=PASSES, i=PACK)
-        wd_raw = [keep.tile([P, PACK, N], F32, name="wd_raw%d" % a, tag="wide%d" % (2 * a), align_bytes=64) for a in range(PASSES)]
+        wd_raw = [
+            laid.tile([P, PACK, N], F32, name="wd_raw%d" % a, offset=SEAM + (a - 1) * 4 * PACK * N, align_bytes=64)
+            for a in range(PASSES)
+        ]
         for a in range(PASSES):
             nc.sync.dma_start(wd_raw[a][:], wvd_rows[a])
 
@@ -117,7 +121,12 @@ def tile_list_engram_dl_tanhLP_kernel(
             )
             nc.vector.quantize_mx(out=wd_codes[a][:].bitcast(FP8X4), scales=wd_scales[a][:], in_=wd_bf[:])
 
-        r_sb = [keep.tile([P, T], F32, name="r_sb%d" % t, tag="wide%d" % t, align_bytes=64) for t in range(PACK)]
+        r_sb = [
+            laid.tile([P, T], F32, name="r_sb0", offset=SEAM - 4 * T, align_bytes=64),
+            keep.tile([P, T], F32, name="r_sb1", tag="wide1", align_bytes=64),
+            laid.tile([P, T], F32, name="r_sb2", offset=SEAM, align_bytes=64),
+            keep.tile([P, T], F32, name="r_sb3", tag="wide3", align_bytes=64),
+        ]
         r_rows = rT.rearrange("(p t) c -> p t c", t=PACK)
         for t in range(PACK):
             nc.sync.dma_start(r_sb[t][:], r_rows[:, t, :])

@@ -22,13 +22,16 @@ PACK = 4
 PASSES = K // (P * PACK)
 BANK = 512
 ROWS = 16
-CHUNKS = [128, 256, 256, 256, 128]
-STORE_CUT = 640
+CHUNKS = [128, 256, 256, 128, 256]
+VALUE_CUT = 640
+WORD_CUTS = [0, 384, 768, J]
 WK_COL = J
 WV_COL = J + N
 PLANE = J + 2 * N
 PICKED_AT = [7 * 1024, 8 * 1024]
 SEAM = 28 * 1024
+WK_RAW_AT = 32 * 1024
+WD_AT = [20 * 1024, 34 * 1024]
 
 
 def tile_list_engram_dl_tanhLP_kernel(
@@ -46,21 +49,21 @@ def tile_list_engram_dl_tanhLP_kernel(
         offsets = keep.tile([P, J // 16], U16, name="offsets")
         tab_sc = keep.tile([P, T], U8, name="tab_sc", tag="pair1", align_bytes=64)
         w_sc = keep.tile([P, 2 * N], U8, name="w_sc", align_bytes=64)
-        planes = keep.tile([P, PASSES, PLANE], U8, name="planes", align_bytes=64)
+        planes = [keep.tile([P, PLANE], U8, name="plane0", align_bytes=64)]
         tab_raw = keep.tile([P, T], I32, name="tab_raw", align_bytes=64)
-        wk_raw = keep.tile([P, PASSES, N], I32, name="wk_raw", align_bytes=64)
+        wk_raw = laid.tile([P, PASSES, N], I32, name="wk_raw", offset=WK_RAW_AT, align_bytes=64)
 
-        nc.scalar.dma_start(w_sc[0:live, 0:N].bitcast(I32), wk_scales.rearrange("a q n -> q a n").bitcast(I32))
-        nc.scalar.dma_start(w_sc[0:live, N : 2 * N].bitcast(I32), wv4_scales.rearrange("a q n -> q a n").bitcast(I32))
+        nc.scalar.dma_start(w_sc[0:live, 0:N].bitcast(I32), wk_scales.rearrange("a q n -> (a q) n").bitcast(I32))
+        nc.scalar.dma_start(w_sc[0:live, N : 2 * N].bitcast(I32), wv4_scales.rearrange("a q n -> (a q) n").bitcast(I32))
         nc.sync.dma_start(offsets[:], offs)
-        nc.sync.dma_start(tab_sc[0:live, :].bitcast(I32), tab_scales.rearrange("a q t -> q a t").bitcast(I32))
+        nc.sync.dma_start(tab_sc[0:live, :].bitcast(I32), tab_scales.rearrange("a q t -> (a q) t").bitcast(I32))
         nc.sync.dma_start(wk_raw[:], wk_words.rearrange("a p n i -> p a (n i)").bitcast(I32))
         nc.sync.dma_start(tab_raw[:], tab_words[0].rearrange("p t b -> p (t b)").bitcast(I32))
 
         for rows in (slice(32, 64), slice(64, P)):
             nc.vector.memset(w_sc[rows, :].bitcast(I32), 0)
             nc.vector.memset(tab_sc[rows, :].bitcast(I32), 0)
-        nc.gpsimd.memset(planes[:].rearrange("p a c -> p (a c)").bitcast(I32), 0)
+        nc.gpsimd.memset(planes[0][:].bitcast(I32), 0)
 
         all_sc = keep.tile([P, PLANE], U8, name="all_sc", align_bytes=64)
         nc.vector.tensor_copy(
@@ -72,22 +75,30 @@ def tile_list_engram_dl_tanhLP_kernel(
         nc.vector.tensor_copy(all_sc[:, 0:J].bitcast(I32), picked_sc[:].bitcast(I32))
         wv_raw = keep.tile([P, PASSES, 2 * N], U8, name="wv_raw", tag="pair1", align_bytes=64)
         nc.sync.dma_start(wv_raw[:].bitcast(I32), wv4_words.rearrange("a p b -> p a b").bitcast(I32))
-        for q in (0, 2, 1, 3):
-            nc.sync.dma_start(planes[32 * q : 32 * q + 4, :, :].bitcast(I32), all_sc[8 * q : 8 * q + 8, :].bitcast(I32))
-
         wvd_rows = wvd.rearrange("(a p i) n -> a p i n", a=PASSES, i=PACK)
         wd_raw = [
-            laid.tile([P, PACK, N], F32, name="wd_raw%d" % a, offset=SEAM + (a - 1) * 4 * PACK * N, align_bytes=64)
+            laid.tile([P, PACK, N], F32, name="wd_raw%d" % a, offset=WD_AT[a], align_bytes=64)
             for a in range(PASSES)
         ]
+
+        def move_rows(a):
+            for r in range(4):
+                rows = all_sc[ROWS * a + r : ROWS * (a + 1) : 4, :]
+                nc.sync.dma_start(planes[a][r:P:32, :].bitcast(I32), rows.bitcast(I32))
+
+        move_rows(0)
         for a in range(PASSES):
             nc.sync.dma_start(wd_raw[a][:], wvd_rows[a])
 
-        wk_codes = keep.tile([P, PASSES, N], I32, name="wk_codes", align_bytes=64)
+        wk_codes = laid.tile([P, PASSES, N], I32, name="wk_codes", offset=SEAM, align_bytes=64)
         nc.vector.tensor_copy(
             wk_codes[:].rearrange("p a (t g m) -> p a g t m", t=PACK, m=4),
             wk_raw[:].rearrange("p a (g m t) -> p a g t m", t=PACK, m=4),
         )
+
+        planes.append(laid.tile([P, PLANE], U8, name="plane1", offset=WK_RAW_AT, align_bytes=64))
+        nc.vector.memset(planes[1][:].bitcast(I32), 0)
+        move_rows(1)
 
         tab_codes = []
         for h in halves:
@@ -124,7 +135,7 @@ def tile_list_engram_dl_tanhLP_kernel(
         r_sb = [
             laid.tile([P, T], F32, name="r_sb0", offset=SEAM - 4 * T, align_bytes=64),
             keep.tile([P, T], F32, name="r_sb1", tag="wide1", align_bytes=64),
-            laid.tile([P, T], F32, name="r_sb2", offset=SEAM, align_bytes=64),
+            laid.tile([P, T], F32, name="r_sb2", offset=WD_AT[1], align_bytes=64),
             keep.tile([P, T], F32, name="r_sb3", tag="wide3", align_bytes=64),
         ]
         r_rows = rT.rearrange("(p t) c -> p t c", t=PACK)
@@ -137,7 +148,7 @@ def tile_list_engram_dl_tanhLP_kernel(
                 lhsT=codes,
                 lhsT_scale=scales,
                 rhs=tab_codes[h][:, a, :].bitcast(FP4X4),
-                rhs_scale=planes[:, a, BANK * h : BANK * (h + 1)],
+                rhs_scale=planes[a][:, BANK * h : BANK * (h + 1)],
                 start=start,
                 stop=stop,
             )
@@ -151,20 +162,22 @@ def tile_list_engram_dl_tanhLP_kernel(
         ke = {}
         ve = {}
 
-        def key(t, h):
+        def key(t, h, passes=range(PASSES)):
             lo, hi = P * t, P * (t + 1)
-            ke[t, h] = psum.tile([P, BANK], F32, name="acc")
-            for a in range(PASSES):
+            for a in passes:
+                if a == 0:
+                    ke[t, h] = psum.tile([P, BANK], F32, name="acc")
                 codes = wk_codes[:, a, lo:hi].bitcast(FP8X4)
-                one_pass(ke[t, h], codes, planes[:, a, WK_COL + lo : WK_COL + hi], a, h, a == 0, a == PASSES - 1)
+                one_pass(ke[t, h], codes, planes[a][:, WK_COL + lo : WK_COL + hi], a, h, a == 0, a == PASSES - 1)
 
-        def base_values(t):
+        def base_values(t, passes=range(PASSES)):
             lo, hi = P * t, P * (t + 1)
             for h in halves:
-                ve[t, h] = psum.tile([P, BANK], F32, name="acc")
-                for a in range(PASSES):
+                for a in passes:
+                    if a == 0:
+                        ve[t, h] = psum.tile([P, BANK], F32, name="acc")
                     codes = wv_codes[:, a, 2 * lo : 2 * hi].bitcast(FP4X4)
-                    one_pass(ve[t, h], codes, planes[:, a, WV_COL + lo : WV_COL + hi], a, h, a == 0, False)
+                    one_pass(ve[t, h], codes, planes[a][:, WV_COL + lo : WV_COL + hi], a, h, a == 0, False)
 
         def change_values(t, a):
             lo, hi = P * t, P * (t + 1)
@@ -184,11 +197,12 @@ def tile_list_engram_dl_tanhLP_kernel(
                 cols = slice(BANK * h, BANK * (h + 1))
                 nc.vector.tensor_tensor(gated[t][:, cols], ve[t, h][:], gate[t][:, cols], MULT)
 
-        for h in halves:
+        for a in range(PASSES):
+            for h in halves:
+                for t in (0, 1):
+                    key(t, h, [a])
             for t in (0, 1):
-                key(t, h)
-        for t in (0, 1):
-            base_values(t)
+                base_values(t, [a])
         for t in (0, 1):
             change_values(t, 0)
         for t in (0, 1):
@@ -215,10 +229,16 @@ def tile_list_engram_dl_tanhLP_kernel(
         out_rows = out_0.rearrange("(p t) j -> p t j", t=PACK)
         out_words = out_1[0].rearrange("p j i -> p (j i)").bitcast(I32)
         pieces = [slice(sum(CHUNKS[:c]), sum(CHUNKS[: c + 1])) for c in range(len(CHUNKS))]
-        stores = {STORE_CUT: slice(0, STORE_CUT), J: slice(STORE_CUT, J)}
 
-        def round_pair(u, c):
-            nc.scalar.copy(y_bf[c][:, :, 2 * u : 2 * u + 2], y[u][:, :, pieces[c]].rearrange("p t j -> p j t"))
+        def round_pair(copy, u, c):
+            copy(y_bf[c][:, :, 2 * u : 2 * u + 2], y[u][:, :, pieces[c]].rearrange("p t j -> p j t"))
+
+        def quantise(c):
+            nc.vector.quantize_mx(
+                out=y_codes[:, pieces[c]].bitcast(FP8X4),
+                scales=y_scales[:, pieces[c]],
+                in_=y_bf[c][:].rearrange("p j t -> p (j t)"),
+            )
 
         whole = slice(0, J)
         values(2)
@@ -231,24 +251,27 @@ def tile_list_engram_dl_tanhLP_kernel(
         add_record(1, whole)
         nc.sync.dma_start(out_rows[:, 0:2, :], y[0][:])
         for c in range(len(CHUNKS)):
-            round_pair(0, c)
+            round_pair(nc.scalar.copy, 0, c)
         add_record(2, whole)
         nc.sync.dma_start(out_rows[:, 2, :], y[1][:, 0, :])
+
         last = PACK - 1
-        for c, cols in enumerate(pieces):
-            add_record(last, cols)
-            if cols.stop in stores:
-                part = stores[cols.stop]
-                nc.sync.dma_start(out_rows[:, last, part], y[1][:, 1, part])
-            round_pair(1, c)
-        for c, cols in enumerate(pieces):
-            nc.vector.quantize_mx(
-                out=y_codes[:, cols].bitcast(FP8X4),
-                scales=y_scales[:, cols],
-                in_=y_bf[c][:].rearrange("p j t -> p (j t)"),
-            )
-            if cols.stop in stores:
-                part = stores[cols.stop]
+        for c in (0, 1, 2):
+            add_record(last, pieces[c])
+            round_pair(nc.scalar.copy, 1, c)
+        nc.sync.dma_start(out_rows[:, last, 0:VALUE_CUT], y[1][:, 1, 0:VALUE_CUT])
+        add_record(last, pieces[4])
+        round_pair(nc.scalar.copy, 1, 4)
+        add_record(last, pieces[3])
+        nc.sync.dma_start(out_rows[:, last, VALUE_CUT:J], y[1][:, 1, VALUE_CUT:J])
+        quantise(0)
+        round_pair(nc.vector.tensor_copy, 1, 3)
+        word_stores = {hi: slice(lo, hi) for lo, hi in zip(WORD_CUTS, WORD_CUTS[1:])}
+        for c in range(1, len(CHUNKS)):
+            quantise(c)
+            if pieces[c].stop in word_stores:
+                part = word_stores[pieces[c].stop]
                 nc.sync.dma_start(out_words[:, part], y_codes[:, part].bitcast(I32))
         for q in range(4):
-            nc.scalar.dma_start(out_2[0, 4 * q : 4 * q + 4, :].bitcast(I32), y_scales[32 * q : 32 * q + 4, :].bitcast(I32))
+            queue = nc.scalar if q % 2 == 0 else nc.sync
+            queue.dma_start(out_2[0, 4 * q : 4 * q + 4, :].bitcast(I32), y_scales[32 * q : 32 * q + 4, :].bitcast(I32))

@@ -42,7 +42,7 @@ def tile_list_engram_dl_tanhLP_kernel(
         keep = ctx.enter_context(tc.tile_pool(name="keep", bufs=1))
         laid = ctx.enter_context(tc.tile_pool(name="laid", bufs=1))
         work = ctx.enter_context(tc.tile_pool(name="work", bufs=4))
-        psum = ctx.enter_context(tc.psum_pool(name="psum", bufs=8))
+        psum = ctx.enter_context(tc.psum_pool(name="psum", bufs=1))
 
         halves = range(J // BANK)
         live = PASSES * ROWS
@@ -126,7 +126,7 @@ def tile_list_engram_dl_tanhLP_kernel(
         wd_scales = [keep.tile([P, N], U8, name="wd_scales%d" % a, align_bytes=64) for a in range(PASSES)]
         for a in range(PASSES):
             wd_bf = keep.tile([P, PACK * N], BF16, name="wd_bf%d" % a, tag="wide%d" % (2 * a + 1), align_bytes=64)
-            nc.scalar.copy(
+            (nc.scalar.copy if a == 0 else nc.vector.tensor_copy)(
                 wd_bf[:].rearrange("p (t m i) -> p m t i", t=PACK, i=PACK),
                 wd_raw[a][:].rearrange("p i (m t) -> p m t i", t=PACK),
             )
@@ -154,7 +154,7 @@ def tile_list_engram_dl_tanhLP_kernel(
             )
 
         gate = [keep.tile([P, J], F32, name="gate%d" % t) for t in range(PACK)]
-        gated = [keep.tile([P, J], F32, name="gated%d" % t) for t in range(PACK)]
+        gated = {}
         y = [
             laid.tile([P, 2, J], F32, name="y0", offset=0, align_bytes=64),
             keep.tile([P, 2, J], F32, name="y1", tag="pair1", align_bytes=64),
@@ -166,7 +166,7 @@ def tile_list_engram_dl_tanhLP_kernel(
             lo, hi = P * t, P * (t + 1)
             for a in passes:
                 if a == 0:
-                    ke[t, h] = psum.tile([P, BANK], F32, name="acc")
+                    ke[t, h] = psum.tile([P, BANK], F32, name="ke", tag="bank%d" % (2 * (t % 2) + h))
                 codes = wk_codes[:, a, lo:hi].bitcast(FP8X4)
                 one_pass(ke[t, h], codes, planes[a][:, WK_COL + lo : WK_COL + hi], a, h, a == 0, a == PASSES - 1)
 
@@ -175,7 +175,7 @@ def tile_list_engram_dl_tanhLP_kernel(
             for h in halves:
                 for a in passes:
                     if a == 0:
-                        ve[t, h] = psum.tile([P, BANK], F32, name="acc")
+                        ve[t, h] = psum.tile([P, BANK], F32, name="ve", tag="bank%d" % ((4 + 2 * t + h) % 8))
                     codes = wv_codes[:, a, 2 * lo : 2 * hi].bitcast(FP4X4)
                     one_pass(ve[t, h], codes, planes[a][:, WV_COL + lo : WV_COL + hi], a, h, a == 0, False)
 
@@ -193,6 +193,7 @@ def tile_list_engram_dl_tanhLP_kernel(
                 nc.scalar.activation(gate[t][:, cols], score[:], TANH)
 
         def gate_values(t):
+            gated[t] = keep.tile([P, J], F32, name="gated%d" % t, tag="gated%d" % (t % 2))
             for h in halves:
                 cols = slice(BANK * h, BANK * (h + 1))
                 nc.vector.tensor_tensor(gated[t][:, cols], ve[t, h][:], gate[t][:, cols], MULT)
@@ -242,13 +243,13 @@ def tile_list_engram_dl_tanhLP_kernel(
 
         whole = slice(0, J)
         values(2)
-        gate_values(0)
         values(3)
+        gate_values(0)
         gate_values(1)
         add_record(0, whole)
         gate_values(2)
-        gate_values(3)
         add_record(1, whole)
+        gate_values(3)
         nc.sync.dma_start(out_rows[:, 0:2, :], y[0][:])
         for c in range(len(CHUNKS)):
             round_pair(nc.scalar.copy, 0, c)

@@ -21,7 +21,6 @@ P = 128
 PACK = 4
 PASSES = K // (P * PACK)
 BANK = 512
-ROWS = 16
 CHUNKS = [128, 256, 256, 128, 256]
 VALUE_CUT = 640
 WORD_CUTS = [0, 384, 768, J]
@@ -29,9 +28,8 @@ WK_COL = J
 WV_COL = J + N
 PLANE = J + 2 * N
 PICKED_AT = [7 * 1024, 8 * 1024]
-SEAM = 28 * 1024
-WK_RAW_AT = 32 * 1024
-WD_AT = [20 * 1024, 34 * 1024]
+ST_AT = [0, 8 * 1024]
+SEAM = 32 * 1024
 
 
 def tile_list_engram_dl_tanhLP_kernel(
@@ -45,61 +43,63 @@ def tile_list_engram_dl_tanhLP_kernel(
         psum = ctx.enter_context(tc.psum_pool(name="psum", bufs=1))
 
         halves = range(J // BANK)
-        live = PASSES * ROWS
         offsets = keep.tile([P, J // 16], U16, name="offsets")
-        tab_sc = keep.tile([P, T], U8, name="tab_sc", tag="pair1", align_bytes=64)
+        tab_sc = keep.tile([P, T], U8, name="tab_sc", align_bytes=64)
         w_sc = keep.tile([P, 2 * N], U8, name="w_sc", align_bytes=64)
-        planes = [keep.tile([P, PLANE], U8, name="plane0", align_bytes=64)]
+        planes = [keep.tile([P, PLANE], U8, name="plane%d" % a, align_bytes=64) for a in range(PASSES)]
         tab_raw = keep.tile([P, T], I32, name="tab_raw", align_bytes=64)
-        wk_raw = laid.tile([P, PASSES, N], I32, name="wk_raw", offset=WK_RAW_AT, align_bytes=64)
+        wk_raw = [keep.tile([P, N], I32, name="wk_raw%d" % a, align_bytes=64) for a in range(PASSES)]
+        wv_raw = [keep.tile([P, 2 * N], U8, name="wv_raw%d" % a, align_bytes=64) for a in range(PASSES)]
 
-        nc.scalar.dma_start(w_sc[0:live, 0:N].bitcast(I32), wk_scales.rearrange("a q n -> (a q) n").bitcast(I32))
-        nc.scalar.dma_start(w_sc[0:live, N : 2 * N].bitcast(I32), wv4_scales.rearrange("a q n -> (a q) n").bitcast(I32))
+        nc.gpsimd.memset(w_sc[:].bitcast(I32), 0)
+        nc.vector.memset(tab_sc[:].bitcast(I32), 0)
+        nc.vector.memset(planes[1][:].bitcast(I32), 0)
+
+        staged = slice(0, P, 4)
         nc.sync.dma_start(offsets[:], offs)
-        nc.sync.dma_start(tab_sc[0:live, :].bitcast(I32), tab_scales.rearrange("a q t -> (a q) t").bitcast(I32))
-        nc.sync.dma_start(wk_raw[:], wk_words.rearrange("a p n i -> p a (n i)").bitcast(I32))
+        for a in range(PASSES):
+            nc.sync.dma_start(wv_raw[a][:].bitcast(I32), wv4_words[a].bitcast(I32))
+        nc.sync.dma_start(tab_sc[staged, :].bitcast(I32), tab_scales.rearrange("a q t -> q a t").bitcast(I32))
+        nc.sync.dma_start(wk_raw[0][:], wk_words[0].rearrange("p n i -> p (n i)").bitcast(I32))
+        nc.scalar.dma_start(w_sc[staged, 0:N].bitcast(I32), wk_scales.rearrange("a q n -> q a n").bitcast(I32))
+        nc.scalar.dma_start(w_sc[staged, N : 2 * N].bitcast(I32), wv4_scales.rearrange("a q n -> q a n").bitcast(I32))
         nc.sync.dma_start(tab_raw[:], tab_words[0].rearrange("p t b -> p (t b)").bitcast(I32))
+        nc.sync.dma_start(wk_raw[1][:], wk_words[1].rearrange("p n i -> p (n i)").bitcast(I32))
 
-        for rows in (slice(32, 64), slice(64, P)):
-            nc.vector.memset(w_sc[rows, :].bitcast(I32), 0)
-            nc.vector.memset(tab_sc[rows, :].bitcast(I32), 0)
-        nc.gpsimd.memset(planes[0][:].bitcast(I32), 0)
-
-        all_sc = keep.tile([P, PLANE], U8, name="all_sc", align_bytes=64)
+        wk_codes = keep.tile([P, PASSES, N], I32, name="wk_codes", align_bytes=64)
+        wv_codes = keep.tile([P, PASSES, 2 * N], U8, name="wv_codes", align_bytes=64)
+        for a in range(PASSES):
+            nc.vector.tensor_copy(
+                wv_codes[:, a, :].bitcast(U16).rearrange("p (t g m) -> p g t m", t=PACK, m=8),
+                wv_raw[a][:].bitcast(U16).rearrange("p (g m t) -> p g t m", t=PACK, m=8),
+            )
         nc.vector.tensor_copy(
-            all_sc[:, J:PLANE].rearrange("p (w t m) -> p w t m", w=2, t=PACK),
+            planes[0][:, J:PLANE].rearrange("p (w t m) -> p w t m", w=2, t=PACK),
             w_sc[:].rearrange("p (w m t) -> p w t m", w=2, t=PACK),
         )
         picked_sc = laid.tile([P, J], U8, name="picked_sc", offset=SEAM - J // 2, align_bytes=64)
         nc.vector.tensor_copy(picked_sc[:], tab_sc[:].indirect(offsets[:]))
-        nc.vector.tensor_copy(all_sc[:, 0:J].bitcast(I32), picked_sc[:].bitcast(I32))
-        wv_raw = keep.tile([P, PASSES, 2 * N], U8, name="wv_raw", tag="pair1", align_bytes=64)
-        nc.sync.dma_start(wv_raw[:].bitcast(I32), wv4_words.rearrange("a p b -> p a b").bitcast(I32))
+        nc.vector.tensor_copy(planes[0][:, 0:J].bitcast(I32), picked_sc[:].bitcast(I32))
+        for a in range(PASSES):
+            nc.vector.tensor_copy(
+                wk_codes[:, a, :].rearrange("p (t g m) -> p g t m", t=PACK, m=4),
+                wk_raw[a][:].rearrange("p (g m t) -> p g t m", t=PACK, m=4),
+            )
+
         wvd_rows = wvd.rearrange("(a p i) n -> a p i n", a=PASSES, i=PACK)
         wd_raw = [
-            laid.tile([P, PACK, N], F32, name="wd_raw%d" % a, offset=WD_AT[a], align_bytes=64)
+            laid.tile([P, PACK, N], F32, name="wd_raw%d" % a, offset=SEAM - 4 * PACK * N * (1 - a), align_bytes=64)
             for a in range(PASSES)
         ]
-
-        def move_rows(a):
-            for r in range(4):
-                rows = all_sc[ROWS * a + r : ROWS * (a + 1) : 4, :]
-                nc.sync.dma_start(planes[a][r:P:32, :].bitcast(I32), rows.bitcast(I32))
-
-        move_rows(0)
         for a in range(PASSES):
+            for r in range(4):
+                if (a, r) != (0, 0):
+                    rows = planes[0][8 * r + 4 * a : P : 32, :]
+                    nc.sync.dma_start(planes[a][r:P:32, :].bitcast(I32), rows.bitcast(I32))
             nc.sync.dma_start(wd_raw[a][:], wvd_rows[a])
 
-        wk_codes = laid.tile([P, PASSES, N], I32, name="wk_codes", offset=SEAM, align_bytes=64)
-        nc.vector.tensor_copy(
-            wk_codes[:].rearrange("p a (t g m) -> p a g t m", t=PACK, m=4),
-            wk_raw[:].rearrange("p a (g m t) -> p a g t m", t=PACK, m=4),
-        )
-
-        planes.append(laid.tile([P, PLANE], U8, name="plane1", offset=WK_RAW_AT, align_bytes=64))
-        nc.vector.memset(planes[1][:].bitcast(I32), 0)
-        move_rows(1)
-
+        st_rows = st.rearrange("(p t) j -> p t j", t=PACK)
+        st_sb = []
         tab_codes = []
         for h in halves:
             picked = laid.tile([P, BANK], U32, name="picked%d" % h, offset=PICKED_AT[h], align_bytes=64)
@@ -110,17 +110,9 @@ def tile_list_engram_dl_tanhLP_kernel(
                 tab_codes[h][:].bitcast(U16).rearrange("p a (g m) -> p g a m", m=8),
                 picked[:].bitcast(U16).rearrange("p (g m a) -> p g a m", a=PASSES, m=8),
             )
-
-        st_rows = st.rearrange("(p t) j -> p t j", t=PACK)
-        st_sb = [laid.tile([P, 2, J], F32, name="st_sb0", offset=0, align_bytes=64)]
-        nc.sync.dma_start(st_sb[0][:], st_rows[:, 0:2, :])
-        wv_codes = keep.tile([P, PASSES, 2 * N], U8, name="wv_codes", align_bytes=64)
-        nc.vector.tensor_copy(
-            wv_codes[:].bitcast(U16).rearrange("p a (t g m) -> p a g t m", t=PACK, m=8),
-            wv_raw[:].bitcast(U16).rearrange("p a (g m t) -> p a g t m", t=PACK, m=8),
-        )
-        st_sb.append(keep.tile([P, 2, J], F32, name="st_sb1", tag="pair1", align_bytes=64))
-        nc.sync.dma_start(st_sb[1][:], st_rows[:, 2:4, :])
+        for u in range(2):
+            st_sb.append(laid.tile([P, 2, J], F32, name="st_sb%d" % u, offset=ST_AT[u], align_bytes=64))
+            nc.sync.dma_start(st_sb[u][:], st_rows[:, 2 * u : 2 * u + 2, :])
 
         wd_codes = [keep.tile([P, N], U32, name="wd_codes%d" % a, align_bytes=64) for a in range(PASSES)]
         wd_scales = [keep.tile([P, N], U8, name="wd_scales%d" % a, align_bytes=64) for a in range(PASSES)]
@@ -135,7 +127,7 @@ def tile_list_engram_dl_tanhLP_kernel(
         r_sb = [
             laid.tile([P, T], F32, name="r_sb0", offset=SEAM - 4 * T, align_bytes=64),
             keep.tile([P, T], F32, name="r_sb1", tag="wide1", align_bytes=64),
-            laid.tile([P, T], F32, name="r_sb2", offset=WD_AT[1], align_bytes=64),
+            laid.tile([P, T], F32, name="r_sb2", offset=SEAM, align_bytes=64),
             keep.tile([P, T], F32, name="r_sb3", tag="wide3", align_bytes=64),
         ]
         r_rows = rT.rearrange("(p t) c -> p t c", t=PACK)
@@ -155,10 +147,7 @@ def tile_list_engram_dl_tanhLP_kernel(
 
         gate = [keep.tile([P, J], F32, name="gate%d" % t) for t in range(PACK)]
         gated = {}
-        y = [
-            laid.tile([P, 2, J], F32, name="y0", offset=0, align_bytes=64),
-            keep.tile([P, 2, J], F32, name="y1", tag="pair1", align_bytes=64),
-        ]
+        y = [laid.tile([P, 2, J], F32, name="y%d" % u, offset=ST_AT[u], align_bytes=64) for u in range(2)]
         ke = {}
         ve = {}
 

@@ -51,20 +51,21 @@ def tile_list_engram_dl_tanhLP_kernel(
         wk_raw = [keep.tile([P, N], I32, name="wk_raw%d" % a, align_bytes=64) for a in range(PASSES)]
         wv_raw = [keep.tile([P, 2 * N], U8, name="wv_raw%d" % a, align_bytes=64) for a in range(PASSES)]
 
-        nc.gpsimd.memset(w_sc[:].bitcast(I32), 0)
+        nc.vector.memset(w_sc[:].bitcast(I32), 0)
         nc.vector.memset(tab_sc[:].bitcast(I32), 0)
         nc.vector.memset(planes[1][:].bitcast(I32), 0)
 
         staged = slice(0, P, 4)
+        wk_rows = wk_words.rearrange("a p n i -> a p (n i)").bitcast(I32)
         nc.sync.dma_start(offsets[:], offs)
-        for a in range(PASSES):
-            nc.sync.dma_start(wv_raw[a][:].bitcast(I32), wv4_words[a].bitcast(I32))
+        nc.sync.dma_start(wv_raw[0][:].bitcast(I32), wv4_words[0].bitcast(I32))
+        nc.sync.dma_start(wk_raw[0][:], wk_rows[0])
+        nc.sync.dma_start(w_sc[staged, 0:N].bitcast(I32), wk_scales.rearrange("a q n -> q a n").bitcast(I32))
+        nc.sync.dma_start(w_sc[staged, N : 2 * N].bitcast(I32), wv4_scales.rearrange("a q n -> q a n").bitcast(I32))
         nc.sync.dma_start(tab_sc[staged, :].bitcast(I32), tab_scales.rearrange("a q t -> q a t").bitcast(I32))
-        nc.sync.dma_start(wk_raw[0][:], wk_words[0].rearrange("p n i -> p (n i)").bitcast(I32))
-        nc.scalar.dma_start(w_sc[staged, 0:N].bitcast(I32), wk_scales.rearrange("a q n -> q a n").bitcast(I32))
-        nc.scalar.dma_start(w_sc[staged, N : 2 * N].bitcast(I32), wv4_scales.rearrange("a q n -> q a n").bitcast(I32))
+        nc.sync.dma_start(wv_raw[1][:].bitcast(I32), wv4_words[1].bitcast(I32))
         nc.sync.dma_start(tab_raw[:], tab_words[0].rearrange("p t b -> p (t b)").bitcast(I32))
-        nc.sync.dma_start(wk_raw[1][:], wk_words[1].rearrange("p n i -> p (n i)").bitcast(I32))
+        nc.sync.dma_start(wk_raw[1][:], wk_rows[1])
 
         wk_codes = keep.tile([P, PASSES, N], I32, name="wk_codes", align_bytes=64)
         wv_codes = keep.tile([P, PASSES, 2 * N], U8, name="wv_codes", align_bytes=64)

@@ -30,6 +30,7 @@ PLANE = J + 2 * N
 PICKED_AT = [7 * 1024, 8 * 1024]
 ST_AT = [0, 8 * 1024]
 SEAM = 32 * 1024
+WD_AT = [16 * 1024, SEAM]
 
 
 def tile_list_engram_dl_tanhLP_kernel(
@@ -48,56 +49,50 @@ def tile_list_engram_dl_tanhLP_kernel(
         w_sc = keep.tile([P, 2 * N], U8, name="w_sc", align_bytes=64)
         planes = [keep.tile([P, PLANE], U8, name="plane%d" % a, align_bytes=64) for a in range(PASSES)]
         tab_raw = keep.tile([P, T], I32, name="tab_raw", align_bytes=64)
-        wk_raw = [keep.tile([P, N], I32, name="wk_raw%d" % a, align_bytes=64) for a in range(PASSES)]
-        wv_raw = [keep.tile([P, 2 * N], U8, name="wv_raw%d" % a, align_bytes=64) for a in range(PASSES)]
+        wk_raw = keep.tile([P, PASSES, N], I32, name="wk_raw", align_bytes=64)
+        wv_raw = keep.tile([P, PASSES, 2 * N], U8, name="wv_raw", align_bytes=64)
 
         nc.vector.memset(w_sc[:].bitcast(I32), 0)
         nc.vector.memset(tab_sc[:].bitcast(I32), 0)
         nc.vector.memset(planes[1][:].bitcast(I32), 0)
 
         staged = slice(0, P, 4)
-        wk_rows = wk_words.rearrange("a p n i -> a p (n i)").bitcast(I32)
         nc.sync.dma_start(offsets[:], offs)
-        nc.sync.dma_start(wv_raw[0][:].bitcast(I32), wv4_words[0].bitcast(I32))
-        nc.sync.dma_start(wk_raw[0][:], wk_rows[0])
+        nc.sync.dma_start(wk_raw[:], wk_words.rearrange("a p n i -> p a (n i)").bitcast(I32))
+        nc.sync.dma_start(wv_raw[:].bitcast(I32), wv4_words.rearrange("a p b -> p a b").bitcast(I32))
         nc.sync.dma_start(w_sc[staged, 0:N].bitcast(I32), wk_scales.rearrange("a q n -> q a n").bitcast(I32))
         nc.sync.dma_start(w_sc[staged, N : 2 * N].bitcast(I32), wv4_scales.rearrange("a q n -> q a n").bitcast(I32))
         nc.sync.dma_start(tab_sc[staged, :].bitcast(I32), tab_scales.rearrange("a q t -> q a t").bitcast(I32))
-        nc.sync.dma_start(wv_raw[1][:].bitcast(I32), wv4_words[1].bitcast(I32))
         nc.sync.dma_start(tab_raw[:], tab_words[0].rearrange("p t b -> p (t b)").bitcast(I32))
-        nc.sync.dma_start(wk_raw[1][:], wk_rows[1])
 
-        wk_codes = keep.tile([P, PASSES, N], I32, name="wk_codes", align_bytes=64)
-        wv_codes = keep.tile([P, PASSES, 2 * N], U8, name="wv_codes", align_bytes=64)
-        for a in range(PASSES):
-            nc.vector.tensor_copy(
-                wv_codes[:, a, :].bitcast(U16).rearrange("p (t g m) -> p g t m", t=PACK, m=8),
-                wv_raw[a][:].bitcast(U16).rearrange("p (g m t) -> p g t m", t=PACK, m=8),
-            )
         nc.vector.tensor_copy(
             planes[0][:, J:PLANE].rearrange("p (w t m) -> p w t m", w=2, t=PACK),
             w_sc[:].rearrange("p (w m t) -> p w t m", w=2, t=PACK),
         )
-        picked_sc = laid.tile([P, J], U8, name="picked_sc", offset=SEAM - J // 2, align_bytes=64)
+        picked_sc = laid.tile([P, J], U8, name="picked_sc", offset=SEAM, align_bytes=64)
         nc.vector.tensor_copy(picked_sc[:], tab_sc[:].indirect(offsets[:]))
         nc.vector.tensor_copy(planes[0][:, 0:J].bitcast(I32), picked_sc[:].bitcast(I32))
-        for a in range(PASSES):
-            nc.vector.tensor_copy(
-                wk_codes[:, a, :].rearrange("p (t g m) -> p g t m", t=PACK, m=4),
-                wk_raw[a][:].rearrange("p (g m t) -> p g t m", t=PACK, m=4),
-            )
+        wk_codes = keep.tile([P, PASSES, N], I32, name="wk_codes", align_bytes=64)
+        nc.vector.tensor_copy(
+            wk_codes[:].rearrange("p a (t g m) -> p a g t m", t=PACK, m=4),
+            wk_raw[:].rearrange("p a (g m t) -> p a g t m", t=PACK, m=4),
+        )
+        wv_codes = keep.tile([P, PASSES, 2 * N], U8, name="wv_codes", align_bytes=64)
+        nc.vector.tensor_copy(
+            wv_codes[:].bitcast(U16).rearrange("p a (t g m) -> p a g t m", t=PACK, m=8),
+            wv_raw[:].bitcast(U16).rearrange("p a (g m t) -> p a g t m", t=PACK, m=8),
+        )
 
         wvd_rows = wvd.rearrange("(a p i) n -> a p i n", a=PASSES, i=PACK)
         wd_raw = [
-            laid.tile([P, PACK, N], F32, name="wd_raw%d" % a, offset=SEAM - 4 * PACK * N * (1 - a), align_bytes=64)
+            laid.tile([P, PACK, N], F32, name="wd_raw%d" % a, offset=WD_AT[a], align_bytes=64)
             for a in range(PASSES)
         ]
         for a in range(PASSES):
-            for r in range(4):
-                if (a, r) != (0, 0):
-                    rows = planes[0][8 * r + 4 * a : P : 32, :]
-                    nc.sync.dma_start(planes[a][r:P:32, :].bitcast(I32), rows.bitcast(I32))
             nc.sync.dma_start(wd_raw[a][:], wvd_rows[a])
+            for r in range(1 - a, 4):
+                rows = planes[0][8 * r + 4 * a : P : 32, :]
+                nc.sync.dma_start(planes[a][r:P:32, :].bitcast(I32), rows.bitcast(I32))
 
         st_rows = st.rearrange("(p t) j -> p t j", t=PACK)
         st_sb = []

@@ -21,7 +21,7 @@ P = 128
 PACK = 4
 PASSES = K // (P * PACK)
 BANK = 512
-CHUNKS = [128, 256, 256, 128, 256]
+CHUNKS = [128, 256, 256, 128, 128, 128]
 VALUE_CUT = 640
 WORD_CUTS = [0, 384, 768, J]
 WK_COL = J
@@ -246,9 +246,9 @@ def tile_list_engram_dl_tanhLP_kernel(
             add_record(last, pieces[c])
             round_pair(nc.scalar.copy, 1, c)
         nc.sync.dma_start(out_rows[:, last, 0:VALUE_CUT], y[1][:, 1, 0:VALUE_CUT])
-        add_record(last, pieces[4])
-        round_pair(nc.scalar.copy, 1, 4)
-        add_record(last, pieces[3])
+        add_record(last, slice(VALUE_CUT, J))
+        for c in (4, 5):
+            round_pair(nc.scalar.copy, 1, c)
         nc.sync.dma_start(out_rows[:, last, VALUE_CUT:J], y[1][:, 1, VALUE_CUT:J])
         quantise(0)
         round_pair(nc.vector.tensor_copy, 1, 3)

from contextlib import ExitStack

import concourse.mybir as mybir

K, N, T, J = 1024, 512, 4096, 1024
FLOPS = 3 * 2 * K * N * J

F32 = mybir.dt.float32
BF16 = mybir.dt.bfloat16
I32 = mybir.dt.int32
U32 = mybir.dt.uint32
U16 = mybir.dt.uint16
U8 = mybir.dt.uint8
FP8X4 = mybir.dt.float8_e4m3fn_x4
FP4X4 = mybir.dt.float4_e2m1fn_x4
MULT = mybir.AluOpType.mult
ADD = mybir.AluOpType.add
TANH = mybir.ActivationFunctionType.Tanh

P = 128
PACK = 4
PASSES = K // (P * PACK)
BANK = 512
CHUNKS = [128, 256, 256, 128, 128, 128]
VALUE_CUT = 640
WORD_CUTS = [0, 384, 768, J]
WK_COL = J
WV_COL = J + N
PLANE = J + 2 * N
PICKED_AT = [7 * 1024, 8 * 1024]
ST_AT = [0, 8 * 1024]
SEAM = 32 * 1024
WD_AT = [16 * 1024, SEAM]


def tile_list_engram_dl_tanhLP_kernel(
    tc, tab_words, tab_scales, wk_words, wk_scales, wv4_words, wv4_scales, wvd, st, rT, offs, out_0, out_1, out_2
):
    nc = tc.nc
    with ExitStack() as ctx:
        keep = ctx.enter_context(tc.tile_pool(name="keep", bufs=1))
        laid = ctx.enter_context(tc.tile_pool(name="laid", bufs=1))
        work = ctx.enter_context(tc.tile_pool(name="work", bufs=4))
        psum = ctx.enter_context(tc.psum_pool(name="psum", bufs=1))

        halves = range(J // BANK)
        offsets = keep.tile([P, J // 16], U16, name="offsets")
        tab_sc = keep.tile([P, T], U8, name="tab_sc", align_bytes=64)
        w_sc = keep.tile([P, 2 * N], U8, name="w_sc", align_bytes=64)
        planes = [keep.tile([P, PLANE], U8, name="plane%d" % a, align_bytes=64) for a in range(PASSES)]
        tab_raw = keep.tile([P, T], I32, name="tab_raw", align_bytes=64)
        wk_raw = keep.tile([P, PASSES, N], I32, name="wk_raw", align_bytes=64)
        wv_raw = keep.tile([P, PASSES, 2 * N], U8, name="wv_raw", align_bytes=64)

        nc.vector.memset(w_sc[:].bitcast(I32), 0)
        nc.vector.memset(tab_sc[:].bitcast(I32), 0)
        nc.vector.memset(planes[1][:].bitcast(I32), 0)

        staged = slice(0, P, 4)
        nc.sync.dma_start(offsets[:], offs)
        nc.sync.dma_start(wk_raw[:], wk_words.rearrange("a p n i -> p a (n i)").bitcast(I32))
        nc.sync.dma_start(wv_raw[:].bitcast(I32), wv4_words.rearrange("a p b -> p a b").bitcast(I32))
        nc.sync.dma_start(w_sc[staged, 0:N].bitcast(I32), wk_scales.rearrange("a q n -> q a n").bitcast(I32))
        nc.sync.dma_start(w_sc[staged, N : 2 * N].bitcast(I32), wv4_scales.rearrange("a q n -> q a n").bitcast(I32))
        nc.sync.dma_start(tab_sc[staged, :].bitcast(I32), tab_scales.rearrange("a q t -> q a t").bitcast(I32))
        nc.sync.dma_start(tab_raw[:], tab_words[0].rearrange("p t b -> p (t b)").bitcast(I32))

        nc.vector.tensor_copy(
            planes[0][:, J:PLANE].rearrange("p (w t m) -> p w t m", w=2, t=PACK),
            w_sc[:].rearrange("p (w m t) -> p w t m", w=2, t=PACK),
        )
        picked_sc = laid.tile([P, J], U8, name="picked_sc", offset=SEAM, align_bytes=64)
        nc.vector.tensor_copy(picked_sc[:], tab_sc[:].indirect(offsets[:]))
        nc.vector.tensor_copy(planes[0][:, 0:J].bitcast(I32), picked_sc[:].bitcast(I32))
        wk_codes = keep.tile([P, PASSES, N], I32, name="wk_codes", align_bytes=64)
        nc.vector.tensor_copy(
            wk_codes[:].rearrange("p a (t g m) -> p a g t m", t=PACK, m=4),
            wk_raw[:].rearrange("p a (g m t) -> p a g t m", t=PACK, m=4),
        )
        wv_codes = keep.tile([P, PASSES, 2 * N], U8, name="wv_codes", align_bytes=64)
        nc.vector.tensor_copy(
            wv_codes[:].bitcast(U16).rearrange("p a (t g m) -> p a g t m", t=PACK, m=8),
            wv_raw[:].bitcast(U16).rearrange("p a (g m t) -> p a g t m", t=PACK, m=8),
        )

        wvd_rows = wvd.rearrange("(a p i) n -> a p i n", a=PASSES, i=PACK)
        wd_raw = [
            laid.tile([P, PACK, N], F32, name="wd_raw%d" % a, offset=WD_AT[a], align_bytes=64)
            for a in range(PASSES)
        ]
        for a in range(PASSES):
            nc.sync.dma_start(wd_raw[a][:], wvd_rows[a])
            for r in range(1 - a, 4):
                rows = planes[0][8 * r + 4 * a : P : 32, :]
                nc.sync.dma_start(planes[a][r:P:32, :].bitcast(I32), rows.bitcast(I32))

        st_rows = st.rearrange("(p t) j -> p t j", t=PACK)
        st_sb = []
        tab_codes = []
        for h in halves:
            picked = laid.tile([P, BANK], U32, name="picked%d" % h, offset=PICKED_AT[h], align_bytes=64)
            picks = offsets[:, BANK // 16 * h : BANK // 16 * (h + 1)]
            nc.vector.tensor_copy(picked[:], tab_raw[:].bitcast(U32).indirect(picks))
            tab_codes.append(keep.tile([P, PASSES, 2 * BANK], U8, name="tab_codes%d" % h, align_bytes=64))
            nc.vector.tensor_copy(
                tab_codes[h][:].bitcast(U16).rearrange("p a (g m) -> p g a m", m=8),
                picked[:].bitcast(U16).rearrange("p (g m a) -> p g a m", a=PASSES, m=8),
            )
        for u in range(2):
            st_sb.append(laid.tile([P, 2, J], F32, name="st_sb%d" % u, offset=ST_AT[u], align_bytes=64))
            nc.sync.dma_start(st_sb[u][:], st_rows[:, 2 * u : 2 * u + 2, :])

        wd_codes = [keep.tile([P, N], U32, name="wd_codes%d" % a, align_bytes=64) for a in range(PASSES)]
        wd_scales = [keep.tile([P, N], U8, name="wd_scales%d" % a, align_bytes=64) for a in range(PASSES)]
        for a in range(PASSES):
            wd_bf = keep.tile([P, PACK * N], BF16, name="wd_bf%d" % a, tag="wide%d" % (2 * a + 1), align_bytes=64)
            (nc.scalar.copy if a == 0 else nc.vector.tensor_copy)(
                wd_bf[:].rearrange("p (t m i) -> p m t i", t=PACK, i=PACK),
                wd_raw[a][:].rearrange("p i (m t) -> p m t i", t=PACK),
            )
            nc.vector.quantize_mx(out=wd_codes[a][:].bitcast(FP8X4), scales=wd_scales[a][:], in_=wd_bf[:])

        r_sb = [
            laid.tile([P, T], F32, name="r_sb0", offset=SEAM - 4 * T, align_bytes=64),
            keep.tile([P, T], F32, name="r_sb1", tag="wide1", align_bytes=64),
            laid.tile([P, T], F32, name="r_sb2", offset=SEAM, align_bytes=64),
            keep.tile([P, T], F32, name="r_sb3", tag="wide3", align_bytes=64),
        ]
        r_rows = rT.rearrange("(p t) c -> p t c", t=PACK)
        for t in range(PACK):
            nc.sync.dma_start(r_sb[t][:], r_rows[:, t, :])

        def one_pass(acc, codes, scales, a, h, start, stop):
            nc.tensor.matmul_mx(
                out=acc[:],
                lhsT=codes,
                lhsT_scale=scales,
                rhs=tab_codes[h][:, a, :].bitcast(FP4X4),
                rhs_scale=planes[a][:, BANK * h : BANK * (h + 1)],
                start=start,
                stop=stop,
            )

        gate = [keep.tile([P, J], F32, name="gate%d" % t) for t in range(PACK)]
        gated = {}
        y = [laid.tile([P, 2, J], F32, name="y%d" % u, offset=ST_AT[u], align_bytes=64) for u in range(2)]
        ke = {}
        ve = {}

        def key(t, h, passes=range(PASSES)):
            lo, hi = P * t, P * (t + 1)
            for a in passes:
                if a == 0:
                    ke[t, h] = psum.tile([P, BANK], F32, name="ke", tag="bank%d" % (2 * (t % 2) + h))
                codes = wk_codes[:, a, lo:hi].bitcast(FP8X4)
                one_pass(ke[t, h], codes, planes[a][:, WK_COL + lo : WK_COL + hi], a, h, a == 0, a == PASSES - 1)

        def base_values(t, passes=range(PASSES)):
            lo, hi = P * t, P * (t + 1)
            for h in halves:
                for a in passes:
                    if a == 0:
                        ve[t, h] = psum.tile([P, BANK], F32, name="ve", tag="bank%d" % ((4 + 2 * t + h) % 8))
                    codes = wv_codes[:, a, 2 * lo : 2 * hi].bitcast(FP4X4)
                    one_pass(ve[t, h], codes, planes[a][:, WV_COL + lo : WV_COL + hi], a, h, a == 0, False)

        def change_values(t, a):
            lo, hi = P * t, P * (t + 1)
            for h in halves:
                codes = wd_codes[a][:, lo:hi].bitcast(FP8X4)
                one_pass(ve[t, h], codes, wd_scales[a][:, lo:hi], a, h, False, a == PASSES - 1)

        def make_gate(t):
            for h in halves:
                cols = slice(BANK * h, BANK * (h + 1))
                score = work.tile([P, BANK], F32, name="score")
                nc.vector.tensor_tensor(score[:], ke[t, h][:], st_sb[t // 2][:, t % 2, cols], MULT)
                nc.scalar.activation(gate[t][:, cols], score[:], TANH)

        def gate_values(t):
            gated[t] = keep.tile([P, J], F32, name="gated%d" % t, tag="gated%d" % (t % 2))
            for h in halves:
                cols = slice(BANK * h, BANK * (h + 1))
                nc.vector.tensor_tensor(gated[t][:, cols], ve[t, h][:], gate[t][:, cols], MULT)

        for a in range(PASSES):
            for h in halves:
                for t in (0, 1):
                    key(t, h, [a])
            for t in (0, 1):
                base_values(t, [a])
        for t in (0, 1):
            change_values(t, 0)
        for t in (0, 1):
            make_gate(t)
            for h in halves:
                key(t + 2, h)
        for t in (0, 1):
            change_values(t, 1)
        for t in (2, 3):
            make_gate(t)

        def values(t):
            base_values(t)
            for a in range(PASSES):
                change_values(t, a)

        def add_record(t, cols):
            picks = offsets[:, cols.start // 16 : cols.stop // 16]
            nc.vector.tensor_tensor(y[t // 2][:, t % 2, cols], r_sb[t][:].indirect(picks), gated[t][:, cols], ADD)

        y_bf = [keep.tile([P, w, PACK], BF16, name="y_bf%d" % c, align_bytes=64) for c, w in enumerate(CHUNKS)]
        y_codes = keep.tile([P, J], U32, name="y_codes", align_bytes=64)
        y_scales = keep.tile([P, J], U8, name="y_scales", align_bytes=64)
        out_rows = out_0.rearrange("(p t) j -> p t j", t=PACK)
        out_words = out_1[0].rearrange("p j i -> p (j i)").bitcast(I32)
        pieces = [slice(sum(CHUNKS[:c]), sum(CHUNKS[: c + 1])) for c in range(len(CHUNKS))]

        def round_pair(copy, u, c):
            copy(y_bf[c][:, :, 2 * u : 2 * u + 2], y[u][:, :, pieces[c]].rearrange("p t j -> p j t"))

        def quantise(c):
            nc.vector.quantize_mx(
                out=y_codes[:, pieces[c]].bitcast(FP8X4),
                scales=y_scales[:, pieces[c]],
                in_=y_bf[c][:].rearrange("p j t -> p (j t)"),
            )

        whole = slice(0, J)
        values(2)
        values(3)
        gate_values(0)
        gate_values(1)
        add_record(0, whole)
        gate_values(2)
        add_record(1, whole)
        gate_values(3)
        nc.sync.dma_start(out_rows[:, 0:2, :], y[0][:])
        for c in range(len(CHUNKS)):
            round_pair(nc.scalar.copy, 0, c)
        add_record(2, whole)
        nc.sync.dma_start(out_rows[:, 2, :], y[1][:, 0, :])

        last = PACK - 1
        for c in (0, 1, 2):
            add_record(last, pieces[c])
            round_pair(nc.scalar.copy, 1, c)
        nc.sync.dma_start(out_rows[:, last, 0:VALUE_CUT], y[1][:, 1, 0:VALUE_CUT])
        add_record(last, slice(VALUE_CUT, J))
        for c in (4, 5):
            round_pair(nc.scalar.copy, 1, c)
        nc.sync.dma_start(out_rows[:, last, VALUE_CUT:J], y[1][:, 1, VALUE_CUT:J])
        quantise(0)
        round_pair(nc.vector.tensor_copy, 1, 3)
        word_stores = {hi: slice(lo, hi) for lo, hi in zip(WORD_CUTS, WORD_CUTS[1:])}
        for c in range(1, len(CHUNKS)):
            quantise(c)
            if pieces[c].stop in word_stores:
                part = word_stores[pieces[c].stop]
                nc.sync.dma_start(out_words[:, part], y_codes[:, part].bitcast(I32))
        for q in range(4):
            queue = nc.scalar if q % 2 == 0 else nc.sync
            queue.dma_start(out_2[0, 4 * q : 4 * q + 4, :].bitcast(I32), y_scales[32 * q : 32 * q + 4, :].bitcast(I32))
